import numpy as np, ml_dtypes
CORES = [16,17,18,19,32,33,34,35]
N = 8
BF = ml_dtypes.bfloat16
def gentries(a):
    return np.ascontiguousarray(a.reshape(8, 16, -1).transpose(0, 2, 1)).reshape(8, -1)
def gtable(e):
    e = np.asarray(e); return np.ascontiguousarray(e.reshape(8, -1, 16).transpose(0, 2, 1)).reshape(128, -1).astype(np.int32)
W, MA, J, P, T = 4096, 128, 768, 3, 3
def lanes(rng, big=False):
    jm = np.zeros((N, 8, MA), np.int64); lab = np.zeros((N, 8, J), np.int64); nx = np.zeros((N, 8, 16, J), np.int64)
    for q in range(N):
        for g in range(8):
            o = rng.permutation(J); p = rng.permutation(MA)
            tail = p[(MA * rng.random(J - MA) ** 2).astype(np.int64)]
            if big: tail[:] = p[0]
            lb = np.concatenate([np.arange(MA), tail]); s = np.argsort(lb, kind="stable"); cnt = np.bincount(lb, minlength=MA); st = np.add.accumulate(cnt) - cnt
            jm[q, g] = o[:MA]; lab[q, g, o] = lb
            nx[q, g][:, o] = o[s[st[lb] + (cnt[lb] * rng.random((16, J))).astype(np.int64)]]
            if big:
                pos = np.zeros(J, np.int64); pos[s] = np.arange(J) - st[lb[s]]
                nx[q, g][:8, o] = o[s[st[lb] + (pos + 1) % cnt[lb]]]
    return jm, lab, nx
def parts(rng, big=False):
    jm, lab, nx = lanes(rng, big); pal = rng.integers(0, W, (8, 16, MA, 6))
    ga = np.arange(8)[None, :, None, None]; ka = np.arange(16)[None, None, :, None]
    tool = np.where(rng.random((N, 8, 16, J)) < 0.75, pal[ga, ka, lab[:, :, None, :], rng.integers(0, 6, (N, 8, 16, J))], rng.integers(0, W, (N, 8, 16, J)))
    sh = (N, 8, 16, P, MA)
    name = np.where(rng.random(sh) < 0.8, pal[ga[..., None], ka[..., None], np.arange(MA), rng.integers(0, 6, sh)], rng.integers(0, W, sh))
    x = np.clip(rng.integers(0, 256, (N, 8, 1, W)) + rng.integers(-64, 65, (N, 8, 16, W)), 0, 255)
    lm = np.clip(rng.integers(64, 257, (N, 8, 1, J)) + rng.integers(-48, 49, (N, 8, 16, J)), 0, 255)
    return {"jm": jm, "nx": nx, "tool": tool, "name": name, "f": rng.integers(0, J, sh), "x": x, "lm": lm, "sd": rng.integers(0, 256, (N, 8, 16, W)), "rt": rng.integers(0, 65, (N, 8, 16, T))}
def full(a):
    return np.ascontiguousarray(a.reshape(N, 128, -1))
def pack(v):
    b = {k: full(v[k]).astype(np.float32).astype(BF) for k in ("x", "sd", "lm", "rt")}
    return {"xw": b["x"], "sd": b["sd"], "jt": full(4096 * v["nx"] + v["tool"]).astype(np.int32), "lm": b["lm"], "rt": b["rt"],
            "pk": full(4096 * v["f"] + v["name"]).astype(np.int32), "jm": np.stack([gtable(a) for a in v["jm"]])}
def setup_inputs(rng):
    return pack(parts(rng))
def setup_inputs_ties(rng):
    v = parts(rng)
    n = rng.choice(np.array([0, 7, 8, 9, 10, 16]), (N, 8, 1, W)); r = np.argsort(rng.random((N, 8, 16, W)), axis=2)
    v["x"] = 100 + (r < n).astype(np.int64); v["lm"] = np.full((N, 8, 16, J), 100); v["rt"] = rng.integers(0, 3, (N, 8, 16, T))
    v["f"] = rng.choice(np.array([0, J // 2, J - 1]), (N, 8, 16, P, MA))
    v["name"][:, :, :, 1] = np.where(rng.random((N, 8, 16, MA)) < 0.5, v["name"][:, :, :, 0], v["name"][:, :, :, 1])
    return pack(v)
def setup_inputs_crowd(rng):
    v = parts(rng); few = rng.integers(0, W, (8, 24)); ga = np.arange(8)[None, :, None, None]; m = np.arange(MA)
    v["tool"] = few[ga, rng.integers(0, 24, (N, 8, 16, J))]; v["name"] = few[ga[..., None], rng.integers(0, 24, (N, 8, 16, P, MA))]
    v["x"] = rng.choice(np.array([0, 3, 7, 8, 9, 128, 250, 254, 255]), (N, 8, 16, W)); v["rt"] = rng.choice(np.array([0, 1, 5, 64]), (N, 8, 16, T))
    other = np.setdiff1d(np.arange(W), few)
    for q in range(N):
        o = rng.permutation(8)
        g = o[0]; c, d = rng.permutation(other)[:2]
        v["lm"][q, g] = 255; v["tool"][q, g] = d; v["name"][q, g] = c; v["f"][q, g][:, 0] = J - 1; v["x"][q, g][:, c] = rng.integers(32, 256, 16)
        for g, w in ((o[1], 0), (o[2], 255)):
            c, d, e = rng.permutation(other)[:3]; m0 = int(rng.integers(1, 9))
            nm = np.where(m < m0, e, c); goes = (m == m0) == (w == 0)
            v["lm"][q, g] = 255; v["x"][q, g] = w; v["name"][q, g][0] = nm
            v["tool"][q, g][0, v["jm"][q, g]] = np.where(goes, nm, d)
            v["rt"][q, g] = rng.integers(17, 65, (16, T)) if w == 0 else rng.integers(0, 3, (16, T))
        g = o[3]; a = rng.permutation(W)[:17]; k0 = rng.integers(1, 8, MA)
        v["x"][q, g][:, a[0]] = rng.integers(0, 150, 16)
        v["x"][q, g][:, a[1:]] = rng.permuted(np.tile(rng.integers(150, 256, (16, 1)), (1, 16)), axis=0)
        v["tool"][q, g][:, v["jm"][q, g]] = np.where(np.arange(16)[:, None] < k0[None, :], a[0], a[1:][:, None])
    return pack(v)
def setup_inputs_ends(rng):
    v = parts(rng, True); e = np.array([0, 1, W - 2, W - 1])
    v["tool"] = np.where(rng.random((N, 8, 16, J)) < 0.5, rng.choice(e, (N, 8, 16, J)), v["tool"])
    v["name"] = np.where(rng.random((N, 8, 16, P, MA)) < 0.5, rng.choice(e, (N, 8, 16, P, MA)), v["name"])
    v["sd"] = np.where(rng.random((N, 8, 16, W)) < 0.5, rng.choice(np.array([0, 1, 255]), (N, 8, 16, W)), v["sd"])
    v["f"] = np.where(rng.random((N, 8, 16, P, MA)) < 0.5, rng.choice(np.array([0, J - 1]), (N, 8, 16, P, MA)), v["f"])
    return pack(v)
def setup_inputs_calm(rng):
    v = parts(rng); q = rng.permutation(N)
    v["lm"][q[0]] = 255; a = np.take_along_axis(v["tool"][q[0]], v["jm"][q[0]][:, None, :], 2)
    np.put_along_axis(v["name"][q[0]], rng.integers(0, P, (8, 16, 1, MA)), a[:, :, None, :], 2)
    v["lm"][q[1]] = 0; v["x"][q[1]] = np.maximum(v["x"][q[1]], 1)
    v["tool"][q[2]] = 2 * (v["tool"][q[2]] // 2); v["sd"][q[2]] = 2 * (v["sd"][q[2]] // 2); v["name"][q[2]] = 2 * (v["name"][q[2]] // 2) + 1
    return pack(v)
def setup_inputs_spread(rng):
    v = parts(rng)
    v["x"] = np.minimum((np.exp2(8 * rng.random((N, 8, 1, W))) * rng.random((N, 8, 16, W))).astype(np.int64), 255)
    v["lm"] = np.minimum((np.exp2(8 * rng.random((N, 8, 1, J))) * rng.random((N, 8, 16, J))).astype(np.int64), 255)
    v["rt"] = np.minimum(np.exp2(6 * rng.random((N, 8, 16, T))).astype(np.int64), 64)
    v["sd"] = np.minimum(np.exp2(8 * rng.random((N, 8, 16, W))).astype(np.int64), 255)
    v["tool"] = np.where(rng.random((N, 8, 16, J)) < 0.5, np.minimum((W * rng.random((N, 8, 16, J)) ** 3).astype(np.int64), W - 1), v["tool"])
    v["f"] = np.minimum((J * rng.random((N, 8, 16, P, MA)) ** 3).astype(np.int64), J - 1)
    return pack(v)
def check_inputs(d):
    bad = []
    for k, hi in (("xw", 255), ("sd", 255), ("lm", 255), ("rt", 64)):
        v = np.asarray(d[k]).astype(np.float64)
        if not np.all((v >= 0) & (v <= hi) & (v == np.floor(v))): bad.append("range of " + k)
    for k in ("jt", "pk"):
        v = np.asarray(d[k]).astype(np.int64)
        if np.min(v) < 0 or np.max(v) > 4096 * J - 1 or np.max(v & 4095) > W - 1: bad.append("range of " + k)
    if np.min(d["jm"]) < 0 or np.max(d["jm"]) > J - 1: bad.append("range of jm")
    if bad: return bad
    ok = True; nx = np.asarray(d["jt"]).astype(np.int64).reshape(N, 8, 16, J) >> 12
    for q in range(N):
        starts = gentries(np.asarray(d["jm"][q])).astype(np.int64)
        for g in range(8):
            fr = starts[g]; lab = np.full(J, -1)
            if len(np.unique(fr)) < MA: ok = False; continue
            lab[fr] = np.arange(MA)
            while len(fr):
                tg = nx[q, g][:, fr].reshape(-1); lb = np.tile(lab[fr], 16); new = lab[tg] < 0
                lab[tg[new]] = lb[new]
                if np.any(lab[tg] != lb): ok = False; break
                fr = np.unique(tg[new])
    if not ok: bad.append("lanes: a job can be reached from the starting jobs of two machines")
    return bad
def reference(xw, sd, jt, lm, rt, pk, jm):
    x = xw.astype(np.int64).reshape(N, 8, 16, W); s = sd.astype(np.int64).reshape(N, 8, 16, W); lim = lm.astype(np.int64).reshape(N, 8, 16, J); wr = rt.astype(np.int64).reshape(N, 8, 16, T)
    tab = jt.astype(np.int64).reshape(N, 8, 16, J); p = pk.astype(np.int64).reshape(N, 8, 16, P, MA)
    j = np.stack([gentries(a) for a in jm]).astype(np.int64)
    qa = np.arange(N)[:, None, None]; ga = np.arange(8)[None, :, None]
    for t in range(T):
        jj = np.ascontiguousarray(np.broadcast_to(j[:, :, None, :], (N, 8, 16, MA)))
        rec = np.take_along_axis(tab, jj, 3); a = rec & 4095; n = rec >> 12
        xa = np.take_along_axis(x, a.reshape(N, 8, 1, 16 * MA), 3).reshape(N, 8, 16, 16, MA)
        over = xa > np.take_along_axis(lim, jj, 3)[:, :, :, None, :]
        cond = np.add.reduce(over.astype(np.int64), axis=2) >= 9
        ks = np.argmax(np.add.reduce(xa, axis=2), axis=2)[:, :, None]
        b = a + np.take_along_axis(s, a, 3); b = np.where(b >= W, b - W, b)
        n2 = np.take_along_axis(tab, n, 3) >> 12
        a = np.where(cond, b, a); n = np.where(cond, n2, n)
        np.put_along_axis(tab, jj, 4096 * n + a, 3)
        eq = (p & 4095) == a[:, :, :, None]; hit = np.any(eq, axis=3)
        slot = np.where(hit, np.argmax(eq, axis=3), np.argmax(p >> 12, axis=3))[:, :, :, None]
        old = np.take_along_axis(p, slot, 3)[:, :, :, 0]
        send = np.where(hit, p[:, :, :, P - 1], old)
        np.put_along_axis(p, slot, (4096 * n + a)[:, :, :, None], 3)
        p[:, :, :, P - 1] = np.roll(send, 1, axis=0)
        v = np.take_along_axis(np.where(hit, a, old & 4095), ks, 2)[:, :, 0]; up = np.take_along_axis(hit, ks, 2)[:, :, 0]
        j = np.take_along_axis(n, ks, 2)[:, :, 0]
        low = np.full((N, 8, W), MA); np.minimum.at(low, (qa, ga, v), np.arange(MA)[None, None, :])
        wears = np.take_along_axis(up, np.minimum(low, MA - 1), 2)[:, :, None]
        x = np.where((low < MA)[:, :, None], np.where(wears, np.minimum(x + wr[:, :, :, t:t + 1], 255), np.maximum(x - 8, 0)), x)
    return {"yx": x.reshape(N, 128, W).astype(np.float32).astype(BF), "yp": p.reshape(N, 128, P * MA).astype(np.float32)}

@@ -1,0 +1,440 @@
+from concourse.mybir import AluOpType as A, ActivationFunctionType as AF
+
+NT = 3
+TRASH = 1024
+PB = ["p%d" % i for i in range(8)]
+SCRATCH = {p: ("psum", [128, 512], "float32") for p in PB}
+WHERE = {}
+
+
+def _own(name, cols, dtype):
+    SCRATCH[name] = ("sbuf", [128, cols], dtype)
+    WHERE[name] = (name, 0, cols)
+
+
+def _arena(buf, dtype, pieces):
+    c = 0
+    for name, w in pieces:
+        WHERE[name] = (buf, c, w)
+        c += (w + 15) // 16 * 16
+    SCRATCH[buf] = ("sbuf", [128, c], dtype)
+
+
+for _n, _w, _d in (("X", 4096 + TRASH, "bfloat16"), ("D", 4096, "bfloat16"), ("LM", 768, "bfloat16"), ("RT", 3, "bfloat16"), ("JT", 768, "int32"),
+                   ("PK", 384, "int32"), ("JM", 8, "int32"), ("TL", 768, "float32"), ("NX", 768, "float32"), ("IB", 768, "int32"), ("IC", 768, "int32"),
+                   ("ONE", 512, "bfloat16"), ("BIG", 512, "bfloat16"), ("TRI", 512, "bfloat16"), ("EYE", 128, "bfloat16"), ("EYE4", 128, "bfloat16"),
+                   ("NEYE", 128, "bfloat16"), ("NEYE8", 128, "bfloat16"), ("G8A", 8, "bfloat16"), ("G8", 8, "bfloat16"), ("BOA", 128, "bfloat16"),
+                   ("BO", 128, "bfloat16"), ("GM", 1024, "bfloat16"), ("NGM", 1024, "bfloat16"), ("CS", 2048, "bfloat16"), ("DI", 2048, "bfloat16"),
+                   ("EX", 2048, "bfloat16"), ("RST", 256, "float32"), ("KC", 256, "bfloat16"), ("GD", 16, "bfloat16"), ("MM", 8, "float32"),
+                   ("RTF", 3, "float32"), ("RT8", 3, "float32"), ("M3", 384, "float32"), ("PF", 384, "int32"), ("PG", 384, "float32"),
+                   ("PM", 384, "int32"), ("YP", 384, "float32")):
+    _own(_n, _w, _d)
+for _t in range(NT):
+    for _n, _w, _d in (("XA", 2048, "bfloat16"), ("OV", 2048, "bfloat16"), ("DG", 2048, "bfloat16"), ("N2", 2048, "float16"), ("GV", 128, "int32"),
+                       ("LAND", 128, "int32")):
+        _own("%s%d" % (_n, _t), _w, _d)
+    SCRATCH["E3%d" % _t] = ("sbuf", [128, 8, 32], "bfloat16")
+    SCRATCH["EE%d" % _t] = ("sbuf", [128, 8, 128], "bfloat16")
+    _arena("u%d" % _t, "uint16", [("%s%d" % (n, _t), w) for n, w in (("JL", 8), ("aL", 128), ("nL", 128), ("VL", 8), ("OF", 8))])
+    _arena("f%d" % _t, "float32", [("%s%d" % (n, _t), w) for n, w in (
+        ("aF", 128), ("nF", 128), ("pm", 256), ("cS", 128), ("nN", 128), ("Uc", 128), ("ms", 128), ("vC", 128), ("dl", 128), ("xg", 128),
+        ("gd", 128), ("qn", 128), ("q", 128), ("q0", 128), ("q1", 128), ("w0", 128), ("w1", 128), ("OFf", 8))])
+    _arena("i%d" % _t, "int32", [("%s%d" % (n, _t), w) for n, w in (("U1", 128), ("U", 128), ("EQ", 128), ("evM", 128), ("evS", 128), ("M", 384), ("Q", 384))])
+    _arena("b%d" % _t, "bfloat16", [("%s%d" % (n, _t), w) for n, w in (("Lj", 128), ("LT", 128), ("OH", 128), ("e", 384), ("r", 256), ("MW", 128), ("xc", 128))])
+    _arena("h%d" % _t, "float16", [("%s%d" % (n, _t), w) for n, w in (("MN", 128), ("MV", 128))])
+_arena("i%d" % NT, "int32", [("Q%d" % NT, 384)])
+SEMAPHORES = ["v", "a", "t", "c"] + ["d%d" % i for i in range(24)] + ["arr%d" % t for t in range(NT)] + ["loc%d" % t for t in range(NT)]
+
+WAKE = 0.10
+CYC = 0.83e-3
+PEC = 0.42e-3
+
+
+def build(ops, g, T):
+    n = len(ops)
+    acc = {}
+    pred = [[] for _ in range(n)]
+    for i, o in enumerate(ops):
+        ps = set()
+        for buf, lo, hi, wr in o["acc"]:
+            lst = acc.setdefault(buf, [])
+            psum = buf in PB
+            for j, lo2, hi2, wr2 in lst:
+                if (lo < hi2 and lo2 < hi and (wr or wr2)) or (psum and ops[j]["q"] != o["q"]):
+                    ps.add(j)
+        for buf, lo, hi, wr in o["acc"]:
+            acc[buf].append((i, lo, hi, wr))
+        ps.discard(i)
+        pred[i] = sorted(ps)
+    succ = [[] for _ in range(n)]
+    for i in range(n):
+        for j in pred[i]:
+            succ[j].append(i)
+    prio = [0.0] * n
+    for i in range(n - 1, -1, -1):
+        prio[i] = ops[i]["cost"] + ops[i]["lat"] + max([prio[s] + WAKE for s in succ[i]] + [0.0])
+    left = [len(p) for p in pred]
+    done = [None] * n
+    free = {}
+    link = [0.0]
+    ready = {i for i in range(n) if not left[i]}
+    order = []
+    while ready:
+        best = None
+        ests = {}
+        for i in ready:
+            q = ops[i]["q"]
+            est = max([free.get(q, 0.0)] + [done[j] + WAKE for j in pred[i]])
+            ests[i] = est
+            if best is None or est < ests[best] or (est == ests[best] and i < best):
+                best = i
+        q = ops[best]["q"]
+        lim = ests[best] + 0.06
+        pick = max((i for i in ready if ops[i]["q"] == q and ests[i] <= lim), key=lambda i: (prio[i], -i))
+        ready.discard(pick)
+        o = ops[pick]
+        st = ests[pick]
+        free[q] = st + o["cost"]
+        if o["kind"] == "dma":
+            link[0] = max(link[0], st + 1.3) + o["bytes"] / 250e3
+            done[pick] = link[0] + 0.7
+        else:
+            done[pick] = st + o["cost"] + o["lat"]
+        o["when"] = (st, done[pick])
+        order.append(pick)
+        for s in succ[pick]:
+            left[s] -= 1
+            if not left[s]:
+                ready.add(s)
+    eng = {"v": g.vector, "a": g.scalar, "t": g.tensor, "c": g, "s": g.sync}
+    known = {q: {} for q in ("v", "a", "t", "c", "s")}
+    count = {q: 0 for q in eng}
+    comp = [None] * n
+    clock = [None] * n
+    total = {}
+    nd = 0
+    for i in order:
+        o = ops[i]
+        q = o["q"]
+        if o["kind"] == "arrive":
+            comp[i] = (o["sem"], o["val"])
+            clock[i] = {}
+            total[o["sem"]] = o["val"]
+            continue
+        kn = known[q]
+        need = {}
+        for j in pred[i]:
+            s, v = comp[j]
+            if kn.get(s, 0) < v and need.get(s, (0, 0))[0] < v:
+                need[s] = (v, j)
+        for s in sorted(need, key=lambda s: -need[s][1]):
+            v, j = need[s]
+            if kn.get(s, 0) >= v:
+                continue
+            eng[q].wait_ge(T.sem[s], v)
+            kn[s] = v
+            for s2, v2 in clock[j].items():
+                if kn.get(s2, 0) < v2:
+                    kn[s2] = v2
+        clock[i] = dict(kn)
+        if o["kind"] == "dma":
+            s = "d%d" % nd
+            nd += 1
+            o["fns"][0](eng[q]).then_inc(T.sem[s], 16)
+            comp[i] = (s, 16)
+        elif o["kind"] == "remote":
+            o["fns"][0](g)
+            comp[i] = (o["sem"], o["val"])
+        else:
+            for f in o["fns"]:
+                f(eng[q]).then_inc(T.sem[q], 1)
+            count[q] += len(o["fns"])
+            comp[i] = (q, count[q])
+        total[comp[i][0]] = comp[i][1]
+    for s in sorted(total):
+        if known["c"].get(s, 0) < total[s]:
+            g.wait_ge(T.sem[s], total[s])
+    return max(d for d in done if d is not None)
+
+
+def rank_program(g, core, T, topo):
+    rank = T.rank_of(core)
+    if rank is None:
+        return
+    nxt = T.cores[(rank + 1) % len(T.cores)]
+    prv = T.cores[(rank - 1) % len(T.cores)]
+    build(make(core, nxt, prv, T, topo), g, T)
+
+
+def make(core, nxt, prv, T, topo):
+    ops = []
+
+    def ap(x):
+        if isinstance(x, str):
+            x = (x,)
+        name, lo, hi = x[0], (x[1] if len(x) > 1 else 0), (x[2] if len(x) > 2 else None)
+        st = x[3] if len(x) > 3 else 1
+        buf, c0, w = WHERE.get(name, (name, 0, 512))
+        hi = w if hi is None else hi
+        return T[buf][:, c0 + lo:c0 + hi:st] if st > 1 else T[buf][:, c0 + lo:c0 + hi]
+
+    def reg(x, wr):
+        if isinstance(x, str):
+            x = (x,)
+        name, lo, hi = x[0], (x[1] if len(x) > 1 else 0), (x[2] if len(x) > 2 else None)
+        if name[:2] in ("E3", "EE"):
+            return (name, 0, 9999, wr) if hi is None else (name, lo, hi, wr)
+        buf, c0, w = WHERE.get(name, (name, 0, 512))
+        hi = w if hi is None else hi
+        return (buf, c0 + lo, c0 + hi, wr)
+
+    def op(q, fns, R, W, cost, kind="op", lat=0.0, **kw):
+        if not isinstance(fns, list):
+            fns = [fns]
+        o = {"q": q, "fns": fns, "acc": [reg(x, False) for x in R] + [reg(x, True) for x in W], "cost": cost, "kind": kind, "lat": lat}
+        o.update(kw)
+        ops.append(o)
+
+    def width(x):
+        if isinstance(x, str):
+            x = (x,)
+        lo = x[1] if len(x) > 1 else 0
+        hi = x[2] if len(x) > 2 and x[2] is not None else WHERE.get(x[0], (0, 0, 512))[2]
+        return (hi - lo + (x[3] if len(x) > 3 else 1) - 1) // (x[3] if len(x) > 3 else 1)
+
+    def isps(x):
+        return (x if isinstance(x, str) else x[0]) in PB
+
+    def tt(out, a, b, o):
+        c = width(a) * (1 if isps(a) or isps(b) else 2)
+        op("v", lambda e: e.tensor_tensor(ap(out), ap(a), ap(b), o), [a, b], [out], 0.05 + max(64, c) * CYC)
+
+    def ts(out, a, s1, o1, s2=None, o2=None):
+        f = (lambda e: e.tensor_scalar(ap(out), ap(a), s1, None, o1)) if o2 is None else (lambda e: e.tensor_scalar(ap(out), ap(a), s1, s2, o1, o2))
+        op("v", f, [a], [out], 0.05 + max(64, width(a)) * CYC)
+
+    def cp(q, out, a):
+        if q == "v":
+            op("v", lambda e: e.tensor_copy(ap(out), ap(a)), [a], [out], 0.05 + max(64, width(a)) * CYC)
+        else:
+            act(out, a, AF.Copy)
+
+    def act(out, a, f, R=(), **kw):
+        op("a", lambda e: e.activation(ap(out), ap(a), f, **{k: (ap(v) if isinstance(v, tuple) else v) for k, v in kw.items()}), [a] + list(R), [out],
+           0.07 + max(64, width(a)) * CYC)
+
+    def gather(q, out, win, w, lst):
+        n = 16 * width(lst)
+        if q == "v":
+            op("v", lambda e: e.tensor_copy(ap(out), T[win][:, 0:w].indirect(ap(lst))), [(win, 0, w), lst], [out], 0.05 + n * 1.5 * CYC)
+        else:
+            op("a", lambda e: e.activation(ap(out), T[win][:, 0:w].indirect(ap(lst)), AF.Copy), [(win, 0, w), lst], [out], 0.065 + n * 1.5 * CYC)
+
+    def scatter(win, w, lst, val):
+        n = 16 * width(lst)
+        op("v", lambda e: e.tensor_copy(T[win][:, 0:w].indirect(ap(lst)), ap(val)), [lst, val], [(win, 0, w)], 0.05 + n * 3 * CYC)
+
+    def mm(out, parts, rd, dep=()):
+        k = len(parts)
+        fns = [(lambda e, i=i, a=a: e.matmul(ap(a[0]), ap(a[1]) if not callable_(a[1]) else a[1][0](), ap(a[2]), i == 0, i == k - 1)) for i, a in enumerate(parts)]
+        cost = sum(max(min(64, 128), width(a[2])) for a in parts) * PEC + 0.01 * k
+        op("t", fns, list(rd), [out], cost)
+
+    def callable_(x):
+        return isinstance(x, list)
+
+    def load(q, dst, src, nbytes):
+        op(q, lambda e: e.dma_start(ap(dst), T[src][:]), [], [dst], 0.06, kind="dma", bytes=nbytes)
+
+    load("s", "JM", "jm", 4096)
+    load("s", "JT", "jt", 128 * 768 * 4)
+    load("a", "LM", "lm", 128 * 768 * 2)
+    load("s", ("X", 0, 4096), "xw", 1 << 20)
+    load("s", "D", "sd", 1 << 20)
+    load("s", "PK", "pk", 128 * 384 * 4)
+    load("a", "RT", "rt", 768)
+
+    def fill(x, val):
+        op("v", lambda e: e.memset(ap(x), val), [], [x], 0.05 + max(64, width(x) * 0.5) * CYC)
+
+    def sel(out, a, pat, base, cm, cmp=A.is_ge):
+        op("c", lambda e: e.affine_select(ap(out), ap(a), pat, cmp, 0.0, base, cm), [a], [out], 0.17 + 2 * width(out) * CYC)
+
+    fill("ONE", 1.0)
+    fill("BIG", 8192.0)
+    sel("EYE", ("ONE", 0, 128), [[-1, 128]], 0, 1, A.is_equal)
+    sel("G8A", ("ONE", 0, 8), [[-16, 8]], 0, 1)
+    sel("G8", "G8A", [[16, 8]], 15, -1)
+    sel("BOA", ("ONE", 0, 128), [[-16, 8], [0, 16]], 0, 1)
+    sel("BO", "BOA", [[16, 8], [0, 16]], 15, -1)
+    op("c", lambda e: e.iota(ap("KC"), [[0, 16], [-1, 16]], 15, 0, allow_small_or_imprecise_dtypes=True), [], ["KC"], 0.13 + 512 * CYC)
+    op("c", lambda e: e.iota(ap("MM"), [[128, 8]], 2048, 1, allow_small_or_imprecise_dtypes=True), [], ["MM"], 0.15)
+    sel("TRI", "BIG", [[0, 4], [-1, 128]], 0, 1)
+    fill("RST", 1.0)
+    fill(("RST", 0, 256, 32), 0.0)
+    fill("CS", 0.0)
+    fill("DI", 0.0)
+    for k in range(16):
+        cp("v", ("EX", k, 2048, 16), "EYE")
+    for k in range(16):
+        cp("v", ("CS", k * 128 + k, k * 128 + 128, 16), "G8")
+    ts(("GD", 0, 16, 2), "G8", 16.0, A.mult)
+    ts(("GD", 1, 16, 2), "G8", 16.0, A.mult)
+    for k in range(16):
+        cp("v", ("DI", k * 128 + k, k * 128 + 128, 16), ("EYE", k, 128, 16))
+    for gg in range(8):
+        op("v", lambda e, gg=gg: e.tensor_scalar(ap(("GM", gg * 128, gg * 128 + 128)), ap(("ONE", 0, 128)), ap(("G8", gg, gg + 1)), None, A.mult),
+           [("ONE", 0, 128), "G8"], [("GM", gg * 128, gg * 128 + 128)], 0.1)
+    act("NGM", "GM", AF.Copy, scale=-1.0)
+    ts("EYE4", "EYE", 4.0, A.mult)
+    ts("NEYE", "EYE", -1.0, A.mult)
+    ts("NEYE8", "EYE", -8.0, A.mult)
+
+    cp("v", "JL0", "JM")
+    ts("IC", "JT", 4095, A.bitwise_and)
+    cp("v", "TL", "IC")
+    ts("IB", "JT", 12, A.logical_shift_right)
+    cp("v", "NX", "IB")
+    cp("v", "RTF", "RT")
+    ts("RT8", "RT", -1.0, A.mult, -8.0, A.add)
+    ts("M0", "PK", 4095, A.bitwise_and)
+    ts("M3", "M0", -3.0, A.mult)
+    for i in range(3):
+        ts(("PG", 128 * i, 128 * i + 128), ("PK", 128 * i, 128 * i + 128), 4.0, A.mult, 4096.0 * (2 - i), A.add)
+    tt("Q0", "PG", "M3", A.add)
+
+    for t in range(NT):
+        def n_(x, t=t):
+            return "%s%d" % (x, t)
+        last = t == NT - 1
+        JL, aL, nL, XA, OV, DG, N2 = (n_(x) for x in ("JL", "aL", "nL", "XA", "OV", "DG", "N2"))
+        Q2 = ("Q0", 256, 384) if t == 0 else "LAND%d" % (t - 1)
+        Q0, Q1 = (n_("Q"), 0, 128), (n_("Q"), 128, 256)
+        gather("v", aL, "TL", 768, JL)
+        gather("a", n_("Lj"), "LM", 768, JL)
+        gather("v", nL, "NX", 768, JL)
+        cp("v", n_("aF"), aL)
+        cp("v", n_("nF"), nL)
+        mm(("p4", 384, 512), [(("p4", 384, 512), n_("Lj"), "EYE")], [n_("Lj"), "EYE"])
+        cp("a", n_("LT"), ("p4", 384, 512))
+        for h in range(2):
+            gather("a", (DG, 1024 * h, 1024 * h + 1024), "D", 4096, (aL, 64 * h, 64 * h + 64))
+        for h in range(2):
+            gather("a", (N2, 1024 * h, 1024 * h + 1024), "NX", 768, (nL, 64 * h, 64 * h + 64))
+        for q, e in enumerate(XQ):
+            gather(e, (XA, 512 * q, 512 * q + 512), "X", 4096, (aL, 32 * q, 32 * q + 32))
+        for q in range(4):
+            c = (XA, 512 * q, 512 * q + 512)
+            b = "p%d" % (q % 2)
+            mm(b, [(b, n_("LT"), ("EX", 512 * q, 512 * q + 512))], [n_("LT"), ("EX", 512 * q, 512 * q + 512)])
+            tt((OV, 512 * q, 512 * q + 512), c, b, A.is_gt)
+        mm(("p4", 0, 256), [(("p4", 0, 256), "EYE", "KC")] + [(("p4", k, 256, 16), (XA, k, 2048, 16), "GD") for k in range(16)], ["EYE", "KC", XA, "GD"])
+        op("v", lambda e, x=n_("pm"): e.tensor_tensor_scan(ap(x), ap("RST"), ap(("p4", 0, 256)), 0.0, A.mult, A.max), ["RST", ("p4", 0, 256)], [n_("pm")], 0.27)
+        op("v", lambda e, t=t: e.tensor_tensor(T["E3%d" % t][:, :, :], ap(("p4", 0, 256)), ap("pm%d" % t), A.is_equal), [("p4", 0, 256), n_("pm")], ["E3%d" % t], 0.27)
+        op("v", lambda e, t=t: e.tensor_copy(ap("OH%d" % t), T["E3%d" % t][:, :, 16:32]), ["E3%d" % t], [n_("OH")], 0.1)
+        OHA = ("p4", 256, 384)
+        mm(OHA, [(OHA, n_("OH"), "EYE")], [n_("OH"), "EYE"])
+        for h in range(2):
+            o = ("p5", 64 * h, 64 * h + 64)
+            mm(o, [(o, ("CS", 128 * k, 128 * k + 128), (OV, 1024 * h + k, 1024 * h + 1024, 16)) for k in range(16)], ["CS", (OV, 1024 * h, 1024 * h + 1024)])
+        ts(n_("cS"), ("p5", 0, 128), 8.5, A.is_ge)
+        mm(("p6", 128, 256), [(("p6", 128, 256), ("DI", 128 * k, 128 * k + 128), (N2, k, 2048, 16)) for k in range(16)], ["DI", N2])
+        mm(("p6", 0, 128), [(("p6", 0, 128), ("DI", 128 * k, 128 * k + 128), (DG, k, 2048, 16)) for k in range(16)], ["DI", DG])
+        tA, tB, tC, tD = (("p7", 128 * i, 128 * i + 128) for i in range(4))
+        tt(tA, ("p6", 128, 256), n_("nF"), A.subtract)
+        tt(tA, n_("cS"), tA, A.mult)
+        tt(n_("nN"), tA, n_("nF"), A.add)
+        if not last:
+            tt(n_("MN"), n_("nN"), OHA, A.mult)
+            mm(("p4", 0, 8), [(("p4", 0, 8), ("CS", 128 * k, 128 * k + 128), (n_("MN"), k, 128, 16)) for k in range(16)], ["CS", n_("MN")])
+            cp("v", "JL%d" % (t + 1), ("p4", 0, 8))
+            scatter("NX", 768, JL, n_("nN"))
+        tt(tB, n_("cS"), ("p6", 0, 128), A.mult)
+        tt(n_("U1"), tB, n_("aF"), A.add)
+        ts(n_("U"), n_("U1"), 4095, A.bitwise_and)
+        if not last:
+            scatter("TL", 768, JL, n_("U"))
+        cp("v", tB, n_("U"))
+        ts(n_("Uc"), n_("U"), -2048.0, A.add)
+        if t:
+            ts((n_("M"), 256, 384), Q2, 4095, A.bitwise_and)
+        tt(tD, Q0, Q1, A.max)
+        tt(n_("EQ"), tD, Q2, A.max)
+        tt((n_("r"), 0, 128), Q0, n_("EQ"), A.is_equal)
+        tt((n_("r"), 128, 256), Q1, n_("EQ"), A.is_equal)
+        ts(n_("evM"), n_("EQ"), 4095, A.bitwise_and)
+        ts(n_("evS"), n_("EQ"), 0xFFCFFF, A.bitwise_and)
+        tt(n_("gd"), n_("evS"), Q2, A.subtract)
+        for i in range(3):
+            tt((n_("e"), 128 * i, 128 * i + 128), (n_("M"), 128 * i, 128 * i + 128), tB, A.is_equal)
+        e0, e1, e2 = ((n_("e"), 128 * i, 128 * i + 128) for i in range(3))
+        r0, r1 = (n_("r"), 0, 128), (n_("r"), 128, 256)
+        o = ("p5", 128, 256)
+        mm(o, [(o, "EYE", e0), (o, "EYE", e1), (o, "EYE", e2)], ["EYE", n_("e")])
+        act(n_("ms"), o, AF.Relu, scale=-1.0, bias=1.0)
+        tt(tC, n_("evM"), tB, A.subtract)
+        tt(tC, n_("ms"), tC, A.mult)
+        tt(n_("vC"), tC, n_("Uc"), A.add)
+        tt(n_("MV"), n_("vC"), OHA, A.mult)
+        tt(n_("MW"), n_("ms"), OHA, A.mult)
+        o = ("p4", 8, 16)
+        vl = [("CS", 128 * k, 128 * k + 128) for k in range(16)]
+        vr = [(n_("MV"), k, 128, 16) for k in range(16)]
+        for b in range(2):
+            o2 = "p%d" % (2 + b)
+            mm(o2, [(o2, "EYE", "TRI"), (o2, n_("MV"), ("NGM", 512 * b, 512 * b + 512))] +
+               [((o2, 128 * x, 128 * x + 128), ("GM", 128 * (4 * b + x), 128 * (4 * b + x) + 128), n_("MV")) for x in range(4)],
+               ["EYE", "TRI", n_("MV"), "NGM", "GM"])
+        mm(o, [(o, vl[k], vr[k]) for k in range(16)], ["CS", n_("MV")])
+        ts(n_("VL"), o, 2048.0, A.add)
+        o = ("p5", 0, 128)
+        mm(o, [(o, "BO", n_("MW"))], ["BO", n_("MW")])
+        op("a", lambda e, t=t: e.activation(ap("dl%d" % t), ap(("p5", 0, 128)), AF.Identity, bias=ap(("RTF", t, t + 1)), scale=ap(("RT8", t, t + 1))),
+           [("p5", 0, 128), "RTF", "RT8"], [n_("dl")], 0.18)
+        for x in range(8):
+            op("v", lambda e, x=x, t=t: e.tensor_scalar(T["EE%d" % t][:, :, 16 * x:16 * x + 16], ap(("p%d" % (2 + x // 4), 128 * (x % 4), 128 * (x % 4) + 128)), 0.0, None, A.is_equal),
+               [("p%d" % (2 + x // 4), 128 * (x % 4), 128 * (x % 4) + 128)], [("EE%d" % t, 16 * x, 16 * x + 16)], 0.16)
+        op("v", lambda e, t=t: e.tensor_tensor(ap("xg%d" % t), T.X[:, 0:4096].indirect(ap("VL%d" % t)), ap("dl%d" % t), A.add), [("X", 0, 4096), n_("VL"), n_("dl")], [n_("xg")], 0.22)
+        ts(n_("xc"), n_("xg"), 0.0, A.max, 255.0, A.min)
+        o = ("p4", 16, 24)
+        mm(o, [(o, vl[k], vr[k]) for k in range(16)] +
+           [(("p4", 16 + c, 17 + c), [lambda c=c, t=t: T["EE%d" % t][:, c, :]], ("BIG", 0, 1)) for c in range(8)], ["CS", n_("MV"), "EE%d" % t, "BIG"])
+        tt(n_("OFf"), o, "MM", A.min)
+        ts(n_("OF"), n_("OFf"), 2048.0, A.add)
+        scatter("X", 4096 + TRASH, n_("OF"), n_("xc"))
+        tt(tD, n_("ms"), n_("gd"), A.mult)
+        tt(n_("GV"), tD, Q2, A.add)
+        eng = topo.engines(core, nxt)[:8]
+        rin = topo.engines(prv, core)[:8]
+        rid, pid = topo.addr(nxt)[:2]
+        op("c", lambda e, t=t, rid=rid, pid=pid, m=sum(1 << x for x in eng): e.remote_dma(T["LAND%d" % t][:], T["GV%d" % t][:], T.sem["arr%d" % t], T.sem["loc%d" % t], pid, rid, m),
+           [n_("GV")], [("SENT%d" % t, 0, 1)], 0.3, kind="remote", lat=2.0, sem="loc%d" % t, val=len(eng))
+        op("z%d" % t, None, [("SENT%d" % t, 0, 1)], ["LAND%d" % t], 0.0, kind="arrive", lat=2.0, sem="arr%d" % t, val=len(rin))
+        act(n_("qn"), n_("nN"), AF.Copy, scale=16384.0)
+        tt(n_("q"), n_("qn"), tB, A.add)
+        act(n_("q0"), n_("q"), AF.Copy, bias=8192.0)
+        act(n_("q1"), n_("q"), AF.Copy, bias=4096.0)
+        o = ("p5", 256, 384)
+        mm(o, [(o, "EYE4", e0), (o, "NEYE", e1), (o, "NEYE", e2), (o, "EYE", r0)], ["EYE4", "NEYE", "EYE", n_("e"), n_("r")])
+        ts(n_("w0"), o, 0.5, A.is_ge)
+        o = ("p5", 384, 512)
+        mm(o, [(o, "NEYE8", e0), (o, "EYE4", e1), (o, "NEYE", e2), (o, "EYE", r1)], ["EYE4", "NEYE8", "NEYE", "EYE", n_("e"), n_("r")])
+        ts(n_("w1"), o, 0.5, A.is_ge)
+        for i, (qq, tx) in enumerate(((Q0, tA), (Q1, tD))):
+            tt(tx, n_("q%d" % i), qq, A.subtract)
+            tt(tx, n_("w%d" % i), tx, A.mult)
+            tt(("Q%d" % (t + 1), 128 * i, 128 * i + 128), tx, qq, A.add)
+        if not last:
+            ts(("M%d" % (t + 1), 0, 256), ("Q%d" % (t + 1), 0, 256), 4095, A.bitwise_and)
+
+    for src, lo, hi in ((("Q%d" % NT, 0, 256), 0, 256), ("LAND%d" % (NT - 1), 256, 384)):
+        ts(("PF", lo, hi), src, 0xFFC000, A.bitwise_and)
+        ts(("PM", lo, hi), src, 4095, A.bitwise_and)
+        ts(("PG", lo, hi), ("PF", lo, hi), 0.25, A.mult)
+        tt(("YP", lo, hi), ("PG", lo, hi), ("PM", lo, hi), A.add)
+    op("s", lambda e: e.dma_start(T.yx[:], ap(("X", 0, 4096))), [("X", 0, 4096)], [("OUTX", 0, 1)], 0.06, kind="dma", bytes=1 << 20)
+    op("s", lambda e: e.dma_start(T.yp[:], ap("YP")), ["YP"], [("OUTP", 0, 1)], 0.06, kind="dma", bytes=128 * 384 * 4)
+    return ops
+
+
+XQ = "vaav"

@@ -24,8 +24,9 @@ for _n, _w, _d in (("X", 4096 + TRASH, "bfloat16"), ("D", 4096, "bfloat16"), ("L
                    ("PK", 384, "int32"), ("JM", 8, "int32"), ("TL", 768, "float32"), ("NX", 768, "float32"), ("IB", 768, "int32"), ("IC", 768, "int32"),
                    ("ONE", 512, "bfloat16"), ("BIG", 512, "bfloat16"), ("TRI", 512, "bfloat16"), ("EYE", 128, "bfloat16"), ("EYE4", 128, "bfloat16"),
                    ("NEYE", 128, "bfloat16"), ("NEYE8", 128, "bfloat16"), ("G8A", 8, "bfloat16"), ("G8", 8, "bfloat16"), ("BOA", 128, "bfloat16"),
-                   ("BO", 128, "bfloat16"), ("GM", 1024, "bfloat16"), ("NGM", 1024, "bfloat16"), ("CS", 2048, "bfloat16"), ("DI", 2048, "bfloat16"),
-                   ("EX", 2048, "bfloat16"), ("RST", 256, "float32"), ("KC", 256, "bfloat16"), ("GD", 16, "bfloat16"), ("MM", 8, "float32"),
+                   ("BO", 128, "bfloat16"), ("GM", 1024, "bfloat16"), ("GMA", 1024, "bfloat16"), ("NGM", 1024, "bfloat16"), ("CS", 144, "bfloat16"),
+                   ("DI", 2048, "bfloat16"), ("EX", 2048, "bfloat16"), ("RST", 256, "float32"), ("KC", 256, "bfloat16"), ("GD", 16, "bfloat16"),
+                   ("MM", 8, "float32"), ("WI", 256, "float32"), ("WS", 256, "float32"), ("WF", 256, "float32"),
                    ("RTF", 3, "float32"), ("RT8", 3, "float32"), ("M3", 384, "float32"), ("PF", 384, "int32"), ("PG", 384, "float32"),
                    ("PM", 384, "int32"), ("YP", 384, "float32")):
     _own(_n, _w, _d)
@@ -37,15 +38,25 @@ for _t in range(NT):
     SCRATCH["EE%d" % _t] = ("sbuf", [128, 8, 128], "bfloat16")
     _arena("u%d" % _t, "uint16", [("%s%d" % (n, _t), w) for n, w in (("JL", 8), ("aL", 128), ("nL", 128), ("VL", 8), ("OF", 8))])
     _arena("f%d" % _t, "float32", [("%s%d" % (n, _t), w) for n, w in (
-        ("aF", 128), ("nF", 128), ("pm", 256), ("cS", 128), ("nN", 128), ("Uc", 128), ("ms", 128), ("vC", 128), ("dl", 128), ("xg", 128),
-        ("gd", 128), ("qn", 128), ("q", 128), ("q0", 128), ("q1", 128), ("w0", 128), ("w1", 128), ("OFf", 8))])
-    _arena("i%d" % _t, "int32", [("%s%d" % (n, _t), w) for n, w in (("U1", 128), ("U", 128), ("EQ", 128), ("evM", 128), ("evS", 128), ("M", 384), ("Q", 384))])
-    _arena("b%d" % _t, "bfloat16", [("%s%d" % (n, _t), w) for n, w in (("Lj", 128), ("LT", 128), ("OH", 128), ("e", 384), ("r", 256), ("MW", 128), ("xc", 128))])
-    _arena("h%d" % _t, "float16", [("%s%d" % (n, _t), w) for n, w in (("MN", 128), ("MV", 128))])
+        ("aF", 128), ("pm", 256), ("cS", 128), ("nN", 128), ("U", 128), ("Uc", 128), ("ms", 128), ("ux", 128), ("y1", 128), ("wr", 128), ("ab", 512),
+        ("VF", 8), ("dl", 128), ("xg", 128), ("qn", 128), ("q", 128), ("w", 256), ("OFa", 8), ("OFb", 8))])
+    _arena("i%d" % _t, "int32", [("%s%d" % (n, _t), w) for n, w in (("EQ", 128), ("evM", 128), ("evS", 128), ("M", 384), ("Q", 384))])
+    _arena("b%d" % _t, "bfloat16", [("%s%d" % (n, _t), w) for n, w in (("Lj", 128), ("LT", 128), ("OH", 128), ("e", 384), ("r", 256), ("MW", 128), ("xc", 128),
+                                                                       ("ws", 128))])
+    _arena("h%d" % _t, "float16", [("%s%d" % (n, _t), w) for n, w in (("MN", 128), ("MV", 128), ("nF", 128))])
 _arena("i%d" % NT, "int32", [("Q%d" % NT, 384)])
 SEMAPHORES = ["v", "a", "t", "c"] + ["d%d" % i for i in range(24)] + ["arr%d" % t for t in range(NT)] + ["loc%d" % t for t in range(NT)]
 
+XQ = ("vaaa", "aaaa", "vaaa")
+DQ = ("aaaa", "aaaa", "vvaa")
+NQ = ("aaav", "aavv", "aaav")
+CQ = ("vv", "vv", "vv")
+EB = ("va", "va", "va")
+ORDER = ("nxd", "dxn", "dnx")
+SEED = 741802
+SPREAD = 1.0
 WAKE = 0.10
+TOL = 0.08
 CYC = 0.83e-3
 PEC = 0.42e-3
 
@@ -53,27 +64,44 @@ PEC = 0.42e-3
 def build(ops, g, T):
     n = len(ops)
     acc = {}
+    chain = {}
+    soft = [None] * n
     pred = [[] for _ in range(n)]
     for i, o in enumerate(ops):
         ps = set()
         for buf, lo, hi, wr in o["acc"]:
-            lst = acc.setdefault(buf, [])
             psum = buf in PB
-            for j, lo2, hi2, wr2 in lst:
+            for j, lo2, hi2, wr2 in acc.setdefault(buf, []):
                 if (lo < hi2 and lo2 < hi and (wr or wr2)) or (psum and ops[j]["q"] != o["q"]):
-                    ps.add(j)
+                    if not (o.get("grp") and o["grp"] == ops[j].get("grp")):
+                        ps.add(j)
         for buf, lo, hi, wr in o["acc"]:
             acc[buf].append((i, lo, hi, wr))
         ps.discard(i)
         pred[i] = sorted(ps)
+        o["pred"] = pred[i]
+        k = o.get("line")
+        if k:
+            soft[i] = chain.get(k)
+            chain[k] = i
     succ = [[] for _ in range(n)]
+    left = [len(p) for p in pred]
     for i in range(n):
         for j in pred[i]:
             succ[j].append(i)
+        if soft[i] is not None and soft[i] not in pred[i]:
+            succ[soft[i]].append(i)
+            left[i] += 1
     prio = [0.0] * n
     for i in range(n - 1, -1, -1):
         prio[i] = ops[i]["cost"] + ops[i]["lat"] + max([prio[s] + WAKE for s in succ[i]] + [0.0])
-    left = [len(p) for p in pred]
+    h = SEED
+    for i in range(n):
+        h = (h * 1103515245 + 12345) % 2147483648
+        if ops[i]["kind"] == "load":
+            prio[i] = 1e6 - 1e3 * i
+        else:
+            prio[i] += SPREAD * (h / 2147483648.0)
     done = [None] * n
     free = {}
     link = [0.0]
@@ -83,31 +111,31 @@ def build(ops, g, T):
         best = None
         ests = {}
         for i in ready:
-            q = ops[i]["q"]
-            est = max([free.get(q, 0.0)] + [done[j] + WAKE for j in pred[i]])
+            est = max([free.get(ops[i]["q"], 0.0)] + [done[j] + WAKE for j in pred[i]])
             ests[i] = est
             if best is None or est < ests[best] or (est == ests[best] and i < best):
                 best = i
         q = ops[best]["q"]
-        lim = ests[best] + 0.06
+        lim = ests[best] + TOL
         pick = max((i for i in ready if ops[i]["q"] == q and ests[i] <= lim), key=lambda i: (prio[i], -i))
         ready.discard(pick)
         o = ops[pick]
         st = ests[pick]
         free[q] = st + o["cost"]
-        if o["kind"] == "dma":
+        if o["kind"] in ("load", "dma"):
             link[0] = max(link[0], st + 1.3) + o["bytes"] / 250e3
             done[pick] = link[0] + 0.7
         else:
             done[pick] = st + o["cost"] + o["lat"]
         o["when"] = (st, done[pick])
+        o["pos"] = len(order)
         order.append(pick)
         for s in succ[pick]:
             left[s] -= 1
             if not left[s]:
                 ready.add(s)
     eng = {"v": g.vector, "a": g.scalar, "t": g.tensor, "c": g, "s": g.sync}
-    known = {q: {} for q in ("v", "a", "t", "c", "s")}
+    known = {q: {} for q in eng}
     count = {q: 0 for q in eng}
     comp = [None] * n
     clock = [None] * n
@@ -137,7 +165,7 @@ def build(ops, g, T):
                 if kn.get(s2, 0) < v2:
                     kn[s2] = v2
         clock[i] = dict(kn)
-        if o["kind"] == "dma":
+        if o["kind"] in ("load", "dma"):
             s = "d%d" % nd
             nd += 1
             o["fns"][0](eng[q]).then_inc(T.sem[s], 16)
@@ -169,96 +197,91 @@ def rank_program(g, core, T, topo):
 def make(core, nxt, prv, T, topo):
     ops = []
 
+    def norm(x):
+        x = (x,) if isinstance(x, str) else x
+        buf, c0, w = WHERE.get(x[0], (x[0], 0, 512))
+        lo, hi = (x[1], x[2]) if len(x) > 1 else (0, w)
+        return buf, c0 + lo, c0 + hi, (x[3] if len(x) > 3 else 1)
+
     def ap(x):
-        if isinstance(x, str):
-            x = (x,)
-        name, lo, hi = x[0], (x[1] if len(x) > 1 else 0), (x[2] if len(x) > 2 else None)
-        st = x[3] if len(x) > 3 else 1
-        buf, c0, w = WHERE.get(name, (name, 0, 512))
-        hi = w if hi is None else hi
-        return T[buf][:, c0 + lo:c0 + hi:st] if st > 1 else T[buf][:, c0 + lo:c0 + hi]
+        if isinstance(x, list):
+            return x[0]()
+        buf, lo, hi, st = norm(x)
+        return T[buf][:, lo:hi:st] if st > 1 else T[buf][:, lo:hi]
 
     def reg(x, wr):
-        if isinstance(x, str):
-            x = (x,)
-        name, lo, hi = x[0], (x[1] if len(x) > 1 else 0), (x[2] if len(x) > 2 else None)
-        if name[:2] in ("E3", "EE"):
-            return (name, 0, 9999, wr) if hi is None else (name, lo, hi, wr)
-        buf, c0, w = WHERE.get(name, (name, 0, 512))
-        hi = w if hi is None else hi
-        return (buf, c0 + lo, c0 + hi, wr)
+        if x[:2] in ("E3", "EE"):
+            return (x, 0, 9999, wr)
+        return norm(x)[:3] + (wr,)
 
     def op(q, fns, R, W, cost, kind="op", lat=0.0, **kw):
-        if not isinstance(fns, list):
-            fns = [fns]
-        o = {"q": q, "fns": fns, "acc": [reg(x, False) for x in R] + [reg(x, True) for x in W], "cost": cost, "kind": kind, "lat": lat}
+        o = {"q": q, "fns": fns if isinstance(fns, list) else [fns], "acc": [reg(x, False) for x in R] + [reg(x, True) for x in W], "cost": cost,
+             "kind": kind, "lat": lat}
         o.update(kw)
         ops.append(o)
 
     def width(x):
-        if isinstance(x, str):
-            x = (x,)
-        lo = x[1] if len(x) > 1 else 0
-        hi = x[2] if len(x) > 2 and x[2] is not None else WHERE.get(x[0], (0, 0, 512))[2]
-        return (hi - lo + (x[3] if len(x) > 3 else 1) - 1) // (x[3] if len(x) > 3 else 1)
+        _, lo, hi, st = norm(x)
+        return (hi - lo + st - 1) // st
 
     def isps(x):
         return (x if isinstance(x, str) else x[0]) in PB
 
+    def vc(c):
+        return 0.05 + max(64, c) * CYC
+
     def tt(out, a, b, o):
-        c = width(a) * (1 if isps(a) or isps(b) else 2)
-        op("v", lambda e: e.tensor_tensor(ap(out), ap(a), ap(b), o), [a, b], [out], 0.05 + max(64, c) * CYC)
+        op("v", lambda e: e.tensor_tensor(ap(out), ap(a), ap(b), o), [a, b], [out], vc(width(a) * (1 if isps(a) or isps(b) else 2)))
 
     def ts(out, a, s1, o1, s2=None, o2=None):
         f = (lambda e: e.tensor_scalar(ap(out), ap(a), s1, None, o1)) if o2 is None else (lambda e: e.tensor_scalar(ap(out), ap(a), s1, s2, o1, o2))
-        op("v", f, [a], [out], 0.05 + max(64, width(a)) * CYC)
+        op("v", f, [a], [out], vc(width(a)))
 
     def cp(q, out, a):
         if q == "v":
-            op("v", lambda e: e.tensor_copy(ap(out), ap(a)), [a], [out], 0.05 + max(64, width(a)) * CYC)
+            op("v", lambda e: e.tensor_copy(ap(out), ap(a)), [a], [out], vc(width(a) * 0.5))
         else:
             act(out, a, AF.Copy)
 
-    def act(out, a, f, R=(), **kw):
-        op("a", lambda e: e.activation(ap(out), ap(a), f, **{k: (ap(v) if isinstance(v, tuple) else v) for k, v in kw.items()}), [a] + list(R), [out],
-           0.07 + max(64, width(a)) * CYC)
+    def act(out, a, f, **kw):
+        op("a", lambda e: e.activation(ap(out), ap(a), f, **kw), [a], [out], 0.07 + max(64, width(a)) * CYC)
 
-    def gather(q, out, win, w, lst):
+    def gather(q, out, win, w, lst, line=None):
         n = 16 * width(lst)
         if q == "v":
-            op("v", lambda e: e.tensor_copy(ap(out), T[win][:, 0:w].indirect(ap(lst))), [(win, 0, w), lst], [out], 0.05 + n * 1.5 * CYC)
+            op("v", lambda e: e.tensor_copy(ap(out), T[win][:, 0:w].indirect(ap(lst))), [(win, 0, w), lst], [out], 0.05 + n * 1.5 * CYC, line=line and line + q)
         else:
-            op("a", lambda e: e.activation(ap(out), T[win][:, 0:w].indirect(ap(lst)), AF.Copy), [(win, 0, w), lst], [out], 0.065 + n * 1.5 * CYC)
+            op("a", lambda e: e.activation(ap(out), T[win][:, 0:w].indirect(ap(lst)), AF.Copy), [(win, 0, w), lst], [out], 0.065 + n * 1.5 * CYC,
+               line=line and line + q)
 
     def scatter(win, w, lst, val):
-        n = 16 * width(lst)
-        op("v", lambda e: e.tensor_copy(T[win][:, 0:w].indirect(ap(lst)), ap(val)), [lst, val], [(win, 0, w)], 0.05 + n * 3 * CYC)
+        op("v", lambda e: e.tensor_copy(T[win][:, 0:w].indirect(ap(lst)), ap(val)), [lst, val], [(win, 0, w)], 0.05 + 16 * width(lst) * 3 * CYC)
 
-    def mm(out, parts, rd, dep=()):
+    def mm(out, parts, rd, start=True, stop=True, each=False, grp=None, line=None):
         k = len(parts)
-        fns = [(lambda e, i=i, a=a: e.matmul(ap(a[0]), ap(a[1]) if not callable_(a[1]) else a[1][0](), ap(a[2]), i == 0, i == k - 1)) for i, a in enumerate(parts)]
-        cost = sum(max(min(64, 128), width(a[2])) for a in parts) * PEC + 0.01 * k
-        op("t", fns, list(rd), [out], cost)
+        fns = [(lambda e, i=i, a=a: e.matmul(ap(a[0]), ap(a[1]), ap(a[2]), each or (start and i == 0), each or (stop and i == k - 1))) for i, a in enumerate(parts)]
+        op("t", fns, list(rd), [out], sum(max(64, width(a[2])) for a in parts) * PEC + 0.01 * k, grp=grp, line=line or grp)
 
-    def callable_(x):
-        return isinstance(x, list)
-
-    def load(q, dst, src, nbytes):
-        op(q, lambda e: e.dma_start(ap(dst), T[src][:]), [], [dst], 0.06, kind="dma", bytes=nbytes)
-
-    load("s", "JM", "jm", 4096)
-    load("s", "JT", "jt", 128 * 768 * 4)
-    load("a", "LM", "lm", 128 * 768 * 2)
-    load("s", ("X", 0, 4096), "xw", 1 << 20)
-    load("s", "D", "sd", 1 << 20)
-    load("s", "PK", "pk", 128 * 384 * 4)
-    load("a", "RT", "rt", 768)
+    def load(dst, src, nbytes, lo=0, hi=None):
+        op("s", lambda e: e.dma_start(ap(dst), T[src][:, lo:hi] if hi else T[src][:]), [], [dst], 0.06, kind="load", bytes=nbytes)
 
     def fill(x, val):
-        op("v", lambda e: e.memset(ap(x), val), [], [x], 0.05 + max(64, width(x) * 0.5) * CYC)
+        op("v", lambda e: e.memset(ap(x), val), [], [x], vc(width(x) * 0.5))
 
     def sel(out, a, pat, base, cm, cmp=A.is_ge):
         op("c", lambda e: e.affine_select(ap(out), ap(a), pat, cmp, 0.0, base, cm), [a], [out], 0.17 + 2 * width(out) * CYC)
+
+    def iota(out, pat, base, cm):
+        op("c", lambda e: e.iota(ap(out), pat, base, cm, allow_small_or_imprecise_dtypes=True), [], [out], 0.13 + 2 * width(out) * CYC)
+
+    load("JM", "jm", 4096)
+    load("JT", "jt", 128 * 768 * 4)
+    load("LM", "lm", 128 * 768 * 2)
+    load("PK", "pk", 128 * 384 * 4)
+    load(("D", 3840, 4096), "sd", 64 << 10, 3840, 4096)
+    load("RT", "rt", 768)
+    load(("X", 0, 4096), "xw", 1 << 20)
+    load(("D", 0, 3840), "sd", 960 << 10, 0, 3840)
 
     fill("ONE", 1.0)
     fill("BIG", 8192.0)
@@ -267,34 +290,45 @@ def make(core, nxt, prv, T, topo):
     sel("G8", "G8A", [[16, 8]], 15, -1)
     sel("BOA", ("ONE", 0, 128), [[-16, 8], [0, 16]], 0, 1)
     sel("BO", "BOA", [[16, 8], [0, 16]], 15, -1)
-    op("c", lambda e: e.iota(ap("KC"), [[0, 16], [-1, 16]], 15, 0, allow_small_or_imprecise_dtypes=True), [], ["KC"], 0.13 + 512 * CYC)
-    op("c", lambda e: e.iota(ap("MM"), [[128, 8]], 2048, 1, allow_small_or_imprecise_dtypes=True), [], ["MM"], 0.15)
+    iota("KC", [[0, 16], [-1, 16]], 15, 0)
+    iota("MM", [[128, 8]], 4096, 1)
     sel("TRI", "BIG", [[0, 4], [-1, 128]], 0, 1)
+    iota("WI", [[1, 256]], 3840, 0)
     fill("RST", 1.0)
     fill(("RST", 0, 256, 32), 0.0)
     fill("CS", 0.0)
+    cp("v", ("CS", 15, 143, 16), "G8")
     fill("DI", 0.0)
     for k in range(16):
         cp("v", ("EX", k, 2048, 16), "EYE")
-    for k in range(16):
-        cp("v", ("CS", k * 128 + k, k * 128 + 128, 16), "G8")
     ts(("GD", 0, 16, 2), "G8", 16.0, A.mult)
     ts(("GD", 1, 16, 2), "G8", 16.0, A.mult)
     for k in range(16):
-        cp("v", ("DI", k * 128 + k, k * 128 + 128, 16), ("EYE", k, 128, 16))
-    for gg in range(8):
-        op("v", lambda e, gg=gg: e.tensor_scalar(ap(("GM", gg * 128, gg * 128 + 128)), ap(("ONE", 0, 128)), ap(("G8", gg, gg + 1)), None, A.mult),
-           [("ONE", 0, 128), "G8"], [("GM", gg * 128, gg * 128 + 128)], 0.1)
+        cp("a", ("DI", k * 128 + k, k * 128 + 128, 16), ("EYE", k, 128, 16))
+    for h in range(2):
+        x = ("GMA", 512 * h, 512 * h + 512)
+        sel(x, "ONE", [[-16, 4], [0, 128]], -64 * h, 1)
+        sel(("GM", 512 * h, 512 * h + 512), x, [[16, 4], [0, 128]], 64 * h + 15, -1)
     act("NGM", "GM", AF.Copy, scale=-1.0)
-    ts("EYE4", "EYE", 4.0, A.mult)
-    ts("NEYE", "EYE", -1.0, A.mult)
-    ts("NEYE8", "EYE", -8.0, A.mult)
+    act("EYE4", "EYE", AF.Copy, scale=4.0)
+    act("NEYE", "EYE", AF.Copy, scale=-1.0)
+    act("NEYE8", "EYE", AF.Copy, scale=-8.0)
+
+    def CS(k):
+        return ("CS", 15 - k, 143 - k)
+
+    def DI(k):
+        return ("DI", 128 * k, 128 * k + 128)
 
     cp("v", "JL0", "JM")
     ts("IC", "JT", 4095, A.bitwise_and)
     cp("v", "TL", "IC")
     ts("IB", "JT", 12, A.logical_shift_right)
     cp("v", "NX", "IB")
+    we = ("D", 3840, 4096)
+    tt("WS", we, "WI", A.add)
+    ts("WF", "WS", 4096.0, A.is_ge, -256.0, A.mult)
+    tt(we, we, "WF", A.add)
     cp("v", "RTF", "RT")
     ts("RT8", "RT", -1.0, A.mult, -8.0, A.add)
     ts("M0", "PK", 4095, A.bitwise_and)
@@ -309,121 +343,157 @@ def make(core, nxt, prv, T, topo):
         last = t == NT - 1
         JL, aL, nL, XA, OV, DG, N2 = (n_(x) for x in ("JL", "aL", "nL", "XA", "OV", "DG", "N2"))
         Q2 = ("Q0", 256, 384) if t == 0 else "LAND%d" % (t - 1)
-        Q0, Q1 = (n_("Q"), 0, 128), (n_("Q"), 128, 256)
+        Q0, Q1, Q01 = (n_("Q"), 0, 128), (n_("Q"), 128, 256), (n_("Q"), 0, 256)
+        tA, tB, tC, tD = (("p7", 128 * i, 128 * i + 128) for i in range(4))
+        tCD = ("p7", 256, 512)
+        OHA = ("p4", 256, 384)
         gather("v", aL, "TL", 768, JL)
         gather("a", n_("Lj"), "LM", 768, JL)
         gather("v", nL, "NX", 768, JL)
-        cp("v", n_("aF"), aL)
-        cp("v", n_("nF"), nL)
-        mm(("p4", 384, 512), [(("p4", 384, 512), n_("Lj"), "EYE")], [n_("Lj"), "EYE"])
-        cp("a", n_("LT"), ("p4", 384, 512))
-        for h in range(2):
-            gather("a", (DG, 1024 * h, 1024 * h + 1024), "D", 4096, (aL, 64 * h, 64 * h + 64))
-        for h in range(2):
-            gather("a", (N2, 1024 * h, 1024 * h + 1024), "NX", 768, (nL, 64 * h, 64 * h + 64))
-        for q, e in enumerate(XQ):
-            gather(e, (XA, 512 * q, 512 * q + 512), "X", 4096, (aL, 32 * q, 32 * q + 32))
+        gather("a", n_("aF"), "TL", 768, JL)
+        gather("a", n_("nF"), "NX", 768, JL)
+        o = ("p4", 384, 512)
+        mm(o, [(o, n_("Lj"), "EYE")], [n_("Lj"), "EYE"])
+        cp("a", n_("LT"), o)
+
+        def wear():
+            for q, e in enumerate(XQ[t]):
+                gather(e, (XA, 512 * q, 512 * q + 512), "X", 4096, (aL, 32 * q, 32 * q + 32), "g%d" % t)
+
+        def dist():
+            for q, e in enumerate(DQ[t]):
+                gather(e, (DG, 512 * q, 512 * q + 512), "D", 4096, (aL, 32 * q, 32 * q + 32), "g%d" % t)
+
+        def second():
+            for q, e in enumerate(NQ[t]):
+                gather(e, (N2, 512 * q, 512 * q + 512), "NX", 768, (nL, 32 * q, 32 * q + 32), "g%d" % t)
+        for y in ORDER[t]:
+            {"d": dist, "n": second, "x": wear}[y]()
         for q in range(4):
-            c = (XA, 512 * q, 512 * q + 512)
-            b = "p%d" % (q % 2)
-            mm(b, [(b, n_("LT"), ("EX", 512 * q, 512 * q + 512))], [n_("LT"), ("EX", 512 * q, 512 * q + 512)])
-            tt((OV, 512 * q, 512 * q + 512), c, b, A.is_gt)
-        mm(("p4", 0, 256), [(("p4", 0, 256), "EYE", "KC")] + [(("p4", k, 256, 16), (XA, k, 2048, 16), "GD") for k in range(16)], ["EYE", "KC", XA, "GD"])
-        op("v", lambda e, x=n_("pm"): e.tensor_tensor_scan(ap(x), ap("RST"), ap(("p4", 0, 256)), 0.0, A.mult, A.max), ["RST", ("p4", 0, 256)], [n_("pm")], 0.27)
-        op("v", lambda e, t=t: e.tensor_tensor(T["E3%d" % t][:, :, :], ap(("p4", 0, 256)), ap("pm%d" % t), A.is_equal), [("p4", 0, 256), n_("pm")], ["E3%d" % t], 0.27)
-        op("v", lambda e, t=t: e.tensor_copy(ap("OH%d" % t), T["E3%d" % t][:, :, 16:32]), ["E3%d" % t], [n_("OH")], 0.1)
-        OHA = ("p4", 256, 384)
+            c, b = (XA, 512 * q, 512 * q + 512), "p%d" % (q // 2)
+            o, x = (OV, 512 * q, 512 * q + 512), ("EX", 512 * q, 512 * q + 512)
+            if CQ[t][q // 2] == "v":
+                mm(b, [(b, n_("LT"), x)], [n_("LT"), x])
+                tt(o, c, b, A.is_gt)
+            else:
+                mm(b, [(b, n_("LT"), x), (b, "NEYE", c)], [n_("LT"), x, "NEYE", c])
+                act(o, b, AF.Sign, scale=-1.0, bias=-0.5)
+        k2 = ("p4", 0, 256)
+        mm(k2, [(k2, "EYE", "KC")] + [(("p4", k, 256, 16), (XA, k, 2048, 16), "GD") for k in range(16)], ["EYE", "KC", XA, "GD"])
+        op("v", lambda e, x=n_("pm"): e.tensor_tensor_scan(ap(x), ap("RST"), ap(("p4", 0, 256)), 0.0, A.mult, A.max), ["RST", k2], [n_("pm")], vc(256))
+        op("v", lambda e, t=t: e.tensor_tensor(T["E3%d" % t][:, :, :], ap(("p4", 0, 256)), ap("pm%d" % t), A.is_equal), [k2, n_("pm")], ["E3%d" % t], vc(256))
+        op("a", lambda e, t=t: e.activation(ap("OH%d" % t), T["E3%d" % t][:, :, 16:32], AF.Copy), ["E3%d" % t], [n_("OH")], 0.18)
         mm(OHA, [(OHA, n_("OH"), "EYE")], [n_("OH"), "EYE"])
         for h in range(2):
             o = ("p5", 64 * h, 64 * h + 64)
-            mm(o, [(o, ("CS", 128 * k, 128 * k + 128), (OV, 1024 * h + k, 1024 * h + 1024, 16)) for k in range(16)], ["CS", (OV, 1024 * h, 1024 * h + 1024)])
-        ts(n_("cS"), ("p5", 0, 128), 8.5, A.is_ge)
-        mm(("p6", 128, 256), [(("p6", 128, 256), ("DI", 128 * k, 128 * k + 128), (N2, k, 2048, 16)) for k in range(16)], ["DI", N2])
-        mm(("p6", 0, 128), [(("p6", 0, 128), ("DI", 128 * k, 128 * k + 128), (DG, k, 2048, 16)) for k in range(16)], ["DI", DG])
-        tA, tB, tC, tD = (("p7", 128 * i, 128 * i + 128) for i in range(4))
-        tt(tA, ("p6", 128, 256), n_("nF"), A.subtract)
-        tt(tA, n_("cS"), tA, A.mult)
+            mm(o, [(o, CS(k), (OV, 1024 * h + k, 1024 * h + 1024, 16)) for k in range(16)], ["CS", (OV, 1024 * h, 1024 * h + 1024)])
+        for h in range(2):
+            ts((n_("cS"), 64 * h, 64 * h + 64), ("p5", 64 * h, 64 * h + 64), 8.5 if CQ[t][h] == "v" else 1.0, A.is_ge)
+
+        def pick_n():
+            for c in range(4):
+                o = ("p6", 128, 256)
+                mm(o, [(o, DI(k), (N2, k, 2048, 16)) for k in range(4 * c, 4 * c + 4)] + ([(o, "NEYE", n_("nF"))] if c == 3 else []),
+                   ["DI", N2] + (["NEYE", n_("nF")] if c == 3 else []), start=c == 0, stop=c == 3, grp="n%d" % t, line="pick%d" % t)
+
+        def pick_d():
+            for c in range(4):
+                o = ("p6", 0, 128)
+                mm(o, [(o, DI(k), (DG, k, 2048, 16)) for k in range(4 * c, 4 * c + 4)], ["DI", DG], start=c == 0, stop=c == 3, grp="d%d" % t, line="pick%d" % t)
+        for f in ((pick_n, pick_d) if t == 0 else (pick_d, pick_n)):
+            f()
+        act(n_("ws"), ("p6", 0, 128), AF.Sign, bias=0.5)
+        act(n_("wr"), n_("ws"), AF.Copy, scale=1920.0, bias=-1920.0)
+        tt(tC, ("p6", 0, 128), n_("wr"), A.add)
+        tt(tA, n_("cS"), ("p6", 128, 256), A.mult)
         tt(n_("nN"), tA, n_("nF"), A.add)
         if not last:
             tt(n_("MN"), n_("nN"), OHA, A.mult)
-            mm(("p4", 0, 8), [(("p4", 0, 8), ("CS", 128 * k, 128 * k + 128), (n_("MN"), k, 128, 16)) for k in range(16)], ["CS", n_("MN")])
+            mm(("p4", 0, 8), [(("p4", 0, 8), CS(k), (n_("MN"), k, 128, 16)) for k in range(16)], ["CS", n_("MN")])
             cp("v", "JL%d" % (t + 1), ("p4", 0, 8))
             scatter("NX", 768, JL, n_("nN"))
-        tt(tB, n_("cS"), ("p6", 0, 128), A.mult)
-        tt(n_("U1"), tB, n_("aF"), A.add)
-        ts(n_("U"), n_("U1"), 4095, A.bitwise_and)
+        tt(tC, n_("cS"), tC, A.mult)
+        tt(tB, tC, n_("aF"), A.add)
+        tt(n_("U"), tC, n_("aF"), A.add)
+        act(n_("Uc"), n_("U"), AF.Identity, bias=-2048.0)
         if not last:
             scatter("TL", 768, JL, n_("U"))
-        cp("v", tB, n_("U"))
-        ts(n_("Uc"), n_("U"), -2048.0, A.add)
         if t:
             ts((n_("M"), 256, 384), Q2, 4095, A.bitwise_and)
         tt(tD, Q0, Q1, A.max)
         tt(n_("EQ"), tD, Q2, A.max)
-        tt((n_("r"), 0, 128), Q0, n_("EQ"), A.is_equal)
-        tt((n_("r"), 128, 256), Q1, n_("EQ"), A.is_equal)
+        r0, r1 = (n_("r"), 0, 128), (n_("r"), 128, 256)
+        tt(r0, Q0, n_("EQ"), A.is_equal)
+        tt(r1, Q1, n_("EQ"), A.is_equal)
         ts(n_("evM"), n_("EQ"), 4095, A.bitwise_and)
         ts(n_("evS"), n_("EQ"), 0xFFCFFF, A.bitwise_and)
-        tt(n_("gd"), n_("evS"), Q2, A.subtract)
-        for i in range(3):
-            tt((n_("e"), 128 * i, 128 * i + 128), (n_("M"), 128 * i, 128 * i + 128), tB, A.is_equal)
+        tt(tD, n_("evS"), Q2, A.subtract)
         e0, e1, e2 = ((n_("e"), 128 * i, 128 * i + 128) for i in range(3))
-        r0, r1 = (n_("r"), 0, 128), (n_("r"), 128, 256)
+        for i, x in enumerate((e0, e1, e2)):
+            tt(x, (n_("M"), 128 * i, 128 * i + 128), tB, A.is_equal)
         o = ("p5", 128, 256)
         mm(o, [(o, "EYE", e0), (o, "EYE", e1), (o, "EYE", e2)], ["EYE", n_("e")])
         act(n_("ms"), o, AF.Relu, scale=-1.0, bias=1.0)
-        tt(tC, n_("evM"), tB, A.subtract)
+        tt(n_("ux"), n_("evM"), tB, A.subtract)
+        tt(tC, n_("ux"), OHA, A.mult)
+        tt(n_("y1"), n_("Uc"), OHA, A.mult)
         tt(tC, n_("ms"), tC, A.mult)
-        tt(n_("vC"), tC, n_("Uc"), A.add)
-        tt(n_("MV"), n_("vC"), OHA, A.mult)
+        tt(n_("MV"), tC, n_("y1"), A.add)
         tt(n_("MW"), n_("ms"), OHA, A.mult)
-        o = ("p4", 8, 16)
-        vl = [("CS", 128 * k, 128 * k + 128) for k in range(16)]
-        vr = [(n_("MV"), k, 128, 16) for k in range(16)]
         for b in range(2):
-            o2 = "p%d" % (2 + b)
-            mm(o2, [(o2, "EYE", "TRI"), (o2, n_("MV"), ("NGM", 512 * b, 512 * b + 512))] +
-               [((o2, 128 * x, 128 * x + 128), ("GM", 128 * (4 * b + x), 128 * (4 * b + x) + 128), n_("MV")) for x in range(4)],
-               ["EYE", "TRI", n_("MV"), "NGM", "GM"])
-        mm(o, [(o, vl[k], vr[k]) for k in range(16)], ["CS", n_("MV")])
+            o = "p%d" % (2 + b)
+            mm(o, [(o, "EYE", "TRI")], ["EYE", "TRI"], stop=False, grp="e%d%d" % (t, b))
+            mm(o, [(o, n_("MV"), ("NGM", 512 * b, 512 * b + 512))] +
+               [((o, 128 * x, 128 * x + 128), ("GM", 128 * (4 * b + x), 128 * (4 * b + x) + 128), n_("MV")) for x in range(4)],
+               [n_("MV"), "NGM", "GM"], start=False, grp="e%d%d" % (t, b))
+        o = ("p4", 8, 16)
+        mm(o, [(o, CS(k), (n_("MV"), k, 128, 16)) for k in range(16)], ["CS", n_("MV")])
         ts(n_("VL"), o, 2048.0, A.add)
+        act(n_("VF"), o, AF.Identity, bias=2048.0)
         o = ("p5", 0, 128)
         mm(o, [(o, "BO", n_("MW"))], ["BO", n_("MW")])
         op("a", lambda e, t=t: e.activation(ap("dl%d" % t), ap(("p5", 0, 128)), AF.Identity, bias=ap(("RTF", t, t + 1)), scale=ap(("RT8", t, t + 1))),
-           [("p5", 0, 128), "RTF", "RT8"], [n_("dl")], 0.18)
+           [o, "RTF", "RT8"], [n_("dl")], 0.18)
         for x in range(8):
-            op("v", lambda e, x=x, t=t: e.tensor_scalar(T["EE%d" % t][:, :, 16 * x:16 * x + 16], ap(("p%d" % (2 + x // 4), 128 * (x % 4), 128 * (x % 4) + 128)), 0.0, None, A.is_equal),
-               [("p%d" % (2 + x // 4), 128 * (x % 4), 128 * (x % 4) + 128)], [("EE%d" % t, 16 * x, 16 * x + 16)], 0.16)
-        op("v", lambda e, t=t: e.tensor_tensor(ap("xg%d" % t), T.X[:, 0:4096].indirect(ap("VL%d" % t)), ap("dl%d" % t), A.add), [("X", 0, 4096), n_("VL"), n_("dl")], [n_("xg")], 0.22)
+            o = ("p%d" % (2 + x // 4), 128 * (x % 4), 128 * (x % 4) + 128)
+            if EB[t][x // 4] == "v":
+                op("v", lambda e, x=x, t=t, o=o: e.tensor_scalar(T["EE%d" % t][:, :, 16 * x:16 * x + 16], ap(o), 0.0, None, A.is_equal), [o], [], 0.16)
+            else:
+                if x % 4 == 0:
+                    act(n_("ab"), "p%d" % (2 + x // 4), AF.Abs)
+                o = (n_("ab"), 128 * (x % 4), 128 * (x % 4) + 128)
+                op("a", lambda e, x=x, t=t, o=o: e.activation(T["EE%d" % t][:, :, 16 * x:16 * x + 16], ap(o), AF.Relu, scale=-1.0, bias=1.0), [o], [], 0.18)
+            ops[-1]["acc"].append(("EE%d" % t, x, x + 1, True))
+        op("v", lambda e, t=t: e.tensor_tensor(ap("xg%d" % t), T.X[:, 0:4096].indirect(ap("VL%d" % t)), ap("dl%d" % t), A.add),
+           [("X", 0, 4096), n_("VL"), n_("dl")], [n_("xg")], 0.22)
         ts(n_("xc"), n_("xg"), 0.0, A.max, 255.0, A.min)
         o = ("p4", 16, 24)
-        mm(o, [(o, vl[k], vr[k]) for k in range(16)] +
-           [(("p4", 16 + c, 17 + c), [lambda c=c, t=t: T["EE%d" % t][:, c, :]], ("BIG", 0, 1)) for c in range(8)], ["CS", n_("MV"), "EE%d" % t, "BIG"])
-        tt(n_("OFf"), o, "MM", A.min)
-        ts(n_("OF"), n_("OFf"), 2048.0, A.add)
+        mm(o, [(("p4", 16 + c, 17 + c), [lambda c=c, t=t: T["EE%d" % t][:, c, :]], ("BIG", 0, 1)) for c in range(8)], ["EE%d" % t, "BIG"], each=True)
+        tt(n_("OFa"), o, "MM", A.min)
+        tt(n_("OFb"), n_("OFa"), n_("VF"), A.max)
+        cp("v", n_("OF"), n_("OFb"))
         scatter("X", 4096 + TRASH, n_("OF"), n_("xc"))
-        tt(tD, n_("ms"), n_("gd"), A.mult)
+        tt(tD, n_("ms"), tD, A.mult)
         tt(n_("GV"), tD, Q2, A.add)
-        eng = topo.engines(core, nxt)[:8]
+        out = topo.engines(core, nxt)[:8]
         rin = topo.engines(prv, core)[:8]
         rid, pid = topo.addr(nxt)[:2]
-        op("c", lambda e, t=t, rid=rid, pid=pid, m=sum(1 << x for x in eng): e.remote_dma(T["LAND%d" % t][:], T["GV%d" % t][:], T.sem["arr%d" % t], T.sem["loc%d" % t], pid, rid, m),
-           [n_("GV")], [("SENT%d" % t, 0, 1)], 0.3, kind="remote", lat=2.0, sem="loc%d" % t, val=len(eng))
+        op("c", lambda e, t=t, rid=rid, pid=pid, m=sum(1 << x for x in out): e.remote_dma(
+            T["LAND%d" % t][:], T["GV%d" % t][:], T.sem["arr%d" % t], T.sem["loc%d" % t], pid, rid, m),
+           [n_("GV")], [("SENT%d" % t, 0, 1)], 0.3, kind="remote", lat=2.0, sem="loc%d" % t, val=len(out))
         op("z%d" % t, None, [("SENT%d" % t, 0, 1)], ["LAND%d" % t], 0.0, kind="arrive", lat=2.0, sem="arr%d" % t, val=len(rin))
         act(n_("qn"), n_("nN"), AF.Copy, scale=16384.0)
         tt(n_("q"), n_("qn"), tB, A.add)
-        act(n_("q0"), n_("q"), AF.Copy, bias=8192.0)
-        act(n_("q1"), n_("q"), AF.Copy, bias=4096.0)
+        act(("p3", 0, 128), n_("q"), AF.Identity, bias=8192.0)
+        act(("p3", 128, 256), n_("q"), AF.Identity, bias=4096.0)
         o = ("p5", 256, 384)
         mm(o, [(o, "EYE4", e0), (o, "NEYE", e1), (o, "NEYE", e2), (o, "EYE", r0)], ["EYE4", "NEYE", "EYE", n_("e"), n_("r")])
-        ts(n_("w0"), o, 0.5, A.is_ge)
         o = ("p5", 384, 512)
         mm(o, [(o, "NEYE8", e0), (o, "EYE4", e1), (o, "NEYE", e2), (o, "EYE", r1)], ["EYE4", "NEYE8", "NEYE", "EYE", n_("e"), n_("r")])
-        ts(n_("w1"), o, 0.5, A.is_ge)
-        for i, (qq, tx) in enumerate(((Q0, tA), (Q1, tD))):
-            tt(tx, n_("q%d" % i), qq, A.subtract)
-            tt(tx, n_("w%d" % i), tx, A.mult)
-            tt(("Q%d" % (t + 1), 128 * i, 128 * i + 128), tx, qq, A.add)
+        ts(n_("w"), ("p5", 256, 512), 0.5, A.is_ge)
+        tt(tCD, ("p3", 0, 256), Q01, A.subtract)
+        tt(tCD, n_("w"), tCD, A.mult)
+        tt(("Q%d" % (t + 1), 0, 256), tCD, Q01, A.add)
         if not last:
             ts(("M%d" % (t + 1), 0, 256), ("Q%d" % (t + 1), 0, 256), 4095, A.bitwise_and)
 
@@ -432,9 +502,6 @@ def make(core, nxt, prv, T, topo):
         ts(("PM", lo, hi), src, 4095, A.bitwise_and)
         ts(("PG", lo, hi), ("PF", lo, hi), 0.25, A.mult)
         tt(("YP", lo, hi), ("PG", lo, hi), ("PM", lo, hi), A.add)
-    op("s", lambda e: e.dma_start(T.yx[:], ap(("X", 0, 4096))), [("X", 0, 4096)], [("OUTX", 0, 1)], 0.06, kind="dma", bytes=1 << 20)
-    op("s", lambda e: e.dma_start(T.yp[:], ap("YP")), ["YP"], [("OUTP", 0, 1)], 0.06, kind="dma", bytes=128 * 384 * 4)
+    op("s", lambda e: e.dma_start(T.yx[:], ap(("X", 0, 4096))), [("X", 0, 4096)], [("OUTX", 0, 1)], 0.06, kind="dma", bytes=1 << 20, lat=7.0)
+    op("s", lambda e: e.dma_start(T.yp[:], ap("YP")), ["YP"], [("OUTP", 0, 1)], 0.06, kind="dma", bytes=128 * 384 * 4, lat=3.0)
     return ops
-
-
-XQ = "vaav"

@@ -22,11 +22,11 @@ def _arena(buf, dtype, pieces):
 
 for _n, _w, _d in (("X", 4096 + TRASH, "bfloat16"), ("D", 4096, "bfloat16"), ("LM", 768, "bfloat16"), ("RT", 3, "bfloat16"), ("JT", 768, "int32"),
                    ("PK", 384, "int32"), ("JM", 8, "int32"), ("TL", 768, "float32"), ("NX", 768, "float32"), ("IB", 768, "int32"), ("IC", 768, "int32"),
-                   ("ONE", 512, "bfloat16"), ("BIG", 512, "bfloat16"), ("TRI", 512, "bfloat16"), ("EYE", 128, "bfloat16"), ("EYE4", 128, "bfloat16"),
-                   ("NEYE", 128, "bfloat16"), ("NEYE8", 128, "bfloat16"), ("G8A", 8, "bfloat16"), ("G8", 8, "bfloat16"), ("BOA", 128, "bfloat16"),
-                   ("BO", 128, "bfloat16"), ("GM", 1024, "bfloat16"), ("GMA", 1024, "bfloat16"), ("NGM", 1024, "bfloat16"), ("CS", 144, "bfloat16"),
-                   ("DI", 2048, "bfloat16"), ("EX", 2048, "bfloat16"), ("RST", 256, "float32"), ("KC", 256, "bfloat16"), ("GD", 16, "bfloat16"),
-                   ("MM", 8, "float32"), ("WI", 256, "float32"), ("WS", 256, "float32"), ("WF", 256, "float32"),
+                   ("ONE", 512, "bfloat16"), ("ZER", 512, "bfloat16"), ("BIG", 512, "bfloat16"), ("TRI", 512, "bfloat16"), ("EYE", 128, "bfloat16"),
+                   ("EYE4", 128, "bfloat16"), ("NEYE", 128, "bfloat16"), ("NEYE8", 128, "bfloat16"), ("G8A", 8, "bfloat16"), ("G8", 8, "bfloat16"),
+                   ("BOA", 128, "bfloat16"), ("BO", 128, "bfloat16"), ("GM", 1024, "bfloat16"), ("GMA", 1024, "bfloat16"), ("NGM", 1024, "bfloat16"),
+                   ("CS", 144, "bfloat16"), ("DI", 2048, "bfloat16"), ("EX", 2048, "bfloat16"), ("RST", 256, "float32"), ("KC", 256, "bfloat16"),
+                   ("GD", 16, "bfloat16"), ("MM", 8, "float32"), ("WI", 256, "float32"), ("WS", 256, "float32"), ("WF", 256, "float32"),
                    ("RTF", 3, "float32"), ("RT8", 3, "float32"), ("M3", 384, "float32"), ("PF", 384, "int32"), ("PG", 384, "float32"),
                    ("PM", 384, "int32"), ("YP", 384, "float32")):
     _own(_n, _w, _d)
@@ -47,14 +47,14 @@ for _t in range(NT):
 _arena("i%d" % NT, "int32", [("Q%d" % NT, 384)])
 SEMAPHORES = ["v", "a", "t", "c"] + ["d%d" % i for i in range(24)] + ["arr%d" % t for t in range(NT)] + ["loc%d" % t for t in range(NT)]
 
-XQ = ("vaaa", "aaaa", "vaaa")
-DQ = ("aaaa", "aaaa", "vvaa")
-NQ = ("aaav", "aavv", "aaav")
-CQ = ("vv", "vv", "vv")
+XQ = ("avaa", "aaaa", "vaaa")
+DQ = ("avva", "aaaa", "aaav")
+NQ = ("vaaa", "aavv", "aaaa")
+CQ = ("aa", "vv", "vv")
 EB = ("va", "va", "va")
-ORDER = ("nxd", "dxn", "dnx")
-SEED = 741802
-SPREAD = 1.0
+ORDER = ("nxd", "dxn", "dxn")
+SEED = 128438
+SPREAD = 0.6
 WAKE = 0.10
 TOL = 0.08
 CYC = 0.83e-3
@@ -257,10 +257,10 @@ def make(core, nxt, prv, T, topo):
     def scatter(win, w, lst, val):
         op("v", lambda e: e.tensor_copy(T[win][:, 0:w].indirect(ap(lst)), ap(val)), [lst, val], [(win, 0, w)], 0.05 + 16 * width(lst) * 3 * CYC)
 
-    def mm(out, parts, rd, start=True, stop=True, each=False, grp=None, line=None):
+    def mm(out, parts, rd, start=True, stop=True, each=False, grp=None):
         k = len(parts)
         fns = [(lambda e, i=i, a=a: e.matmul(ap(a[0]), ap(a[1]), ap(a[2]), each or (start and i == 0), each or (stop and i == k - 1))) for i, a in enumerate(parts)]
-        op("t", fns, list(rd), [out], sum(max(64, width(a[2])) for a in parts) * PEC + 0.01 * k, grp=grp, line=line or grp)
+        op("t", fns, list(rd), [out], sum(max(64, width(a[2])) for a in parts) * PEC + 0.01 * k, grp=grp, line=grp)
 
     def load(dst, src, nbytes, lo=0, hi=None):
         op("s", lambda e: e.dma_start(ap(dst), T[src][:, lo:hi] if hi else T[src][:]), [], [dst], 0.06, kind="load", bytes=nbytes)
@@ -268,19 +268,19 @@ def make(core, nxt, prv, T, topo):
     def fill(x, val):
         op("v", lambda e: e.memset(ap(x), val), [], [x], vc(width(x) * 0.5))
 
-    def sel(out, a, pat, base, cm, cmp=A.is_ge):
-        op("c", lambda e: e.affine_select(ap(out), ap(a), pat, cmp, 0.0, base, cm), [a], [out], 0.17 + 2 * width(out) * CYC)
+    def sel(out, a, pat, base, cm, cmp=A.is_ge, other=0.0):
+        op("c", lambda e: e.affine_select(ap(out), ap(a), pat, cmp, other, base, cm), [a], [out], 0.17 + 2 * width(out) * CYC)
 
     def iota(out, pat, base, cm):
         op("c", lambda e: e.iota(ap(out), pat, base, cm, allow_small_or_imprecise_dtypes=True), [], [out], 0.13 + 2 * width(out) * CYC)
 
     load("JM", "jm", 4096)
     load("JT", "jt", 128 * 768 * 4)
-    load("LM", "lm", 128 * 768 * 2)
-    load("PK", "pk", 128 * 384 * 4)
     load(("D", 3840, 4096), "sd", 64 << 10, 3840, 4096)
     load("RT", "rt", 768)
+    load("LM", "lm", 128 * 768 * 2)
     load(("X", 0, 4096), "xw", 1 << 20)
+    load("PK", "pk", 128 * 384 * 4)
     load(("D", 0, 3840), "sd", 960 << 10, 0, 3840)
 
     fill("ONE", 1.0)
@@ -299,8 +299,9 @@ def make(core, nxt, prv, T, topo):
     fill("CS", 0.0)
     cp("v", ("CS", 15, 143, 16), "G8")
     fill("DI", 0.0)
-    for k in range(16):
-        cp("v", ("EX", k, 2048, 16), "EYE")
+    fill("ZER", 0.0)
+    for h in range(4):
+        sel(("EX", 512 * h, 512 * h + 512), "ZER", [[-1, 32], [0, 16]], -32 * h, 1, A.not_equal, 1.0)
     ts(("GD", 0, 16, 2), "G8", 16.0, A.mult)
     ts(("GD", 1, 16, 2), "G8", 16.0, A.mult)
     for k in range(16):
@@ -352,7 +353,7 @@ def make(core, nxt, prv, T, topo):
         gather("v", nL, "NX", 768, JL)
         gather("a", n_("aF"), "TL", 768, JL)
         gather("a", n_("nF"), "NX", 768, JL)
-        o = ("p4", 384, 512)
+        o = ("p0", 0, 128)
         mm(o, [(o, n_("Lj"), "EYE")], [n_("Lj"), "EYE"])
         cp("a", n_("LT"), o)
 
@@ -379,7 +380,8 @@ def make(core, nxt, prv, T, topo):
                 mm(b, [(b, n_("LT"), x), (b, "NEYE", c)], [n_("LT"), x, "NEYE", c])
                 act(o, b, AF.Sign, scale=-1.0, bias=-0.5)
         k2 = ("p4", 0, 256)
-        mm(k2, [(k2, "EYE", "KC")] + [(("p4", k, 256, 16), (XA, k, 2048, 16), "GD") for k in range(16)], ["EYE", "KC", XA, "GD"])
+        mm(k2, [(k2, "EYE", "KC")], ["EYE", "KC"], stop=False, grp="k%d" % t)
+        mm(k2, [(("p4", k, 256, 16), (XA, k, 2048, 16), "GD") for k in range(16)], [XA, "GD"], start=False, grp="k%d" % t)
         op("v", lambda e, x=n_("pm"): e.tensor_tensor_scan(ap(x), ap("RST"), ap(("p4", 0, 256)), 0.0, A.mult, A.max), ["RST", k2], [n_("pm")], vc(256))
         op("v", lambda e, t=t: e.tensor_tensor(T["E3%d" % t][:, :, :], ap(("p4", 0, 256)), ap("pm%d" % t), A.is_equal), [k2, n_("pm")], ["E3%d" % t], vc(256))
         op("a", lambda e, t=t: e.activation(ap("OH%d" % t), T["E3%d" % t][:, :, 16:32], AF.Copy), ["E3%d" % t], [n_("OH")], 0.18)
@@ -391,21 +393,21 @@ def make(core, nxt, prv, T, topo):
             ts((n_("cS"), 64 * h, 64 * h + 64), ("p5", 64 * h, 64 * h + 64), 8.5 if CQ[t][h] == "v" else 1.0, A.is_ge)
 
         def pick_n():
-            for c in range(4):
-                o = ("p6", 128, 256)
-                mm(o, [(o, DI(k), (N2, k, 2048, 16)) for k in range(4 * c, 4 * c + 4)] + ([(o, "NEYE", n_("nF"))] if c == 3 else []),
-                   ["DI", N2] + (["NEYE", n_("nF")] if c == 3 else []), start=c == 0, stop=c == 3, grp="n%d" % t, line="pick%d" % t)
+            for h in range(2):
+                o = ("p2", 64 * h, 64 * h + 64)
+                mm(o, [(o, DI(k), (N2, 1024 * h + k, 1024 * h + 1024, 16)) for k in range(16)] + [(o, "NEYE", (n_("nF"), 64 * h, 64 * h + 64))],
+                   ["DI", (N2, 1024 * h, 1024 * h + 1024), "NEYE", n_("nF")])
 
         def pick_d():
-            for c in range(4):
-                o = ("p6", 0, 128)
-                mm(o, [(o, DI(k), (DG, k, 2048, 16)) for k in range(4 * c, 4 * c + 4)], ["DI", DG], start=c == 0, stop=c == 3, grp="d%d" % t, line="pick%d" % t)
+            for h in range(2):
+                o = ("p6", 64 * h, 64 * h + 64)
+                mm(o, [(o, DI(k), (DG, 1024 * h + k, 1024 * h + 1024, 16)) for k in range(16)], ["DI", (DG, 1024 * h, 1024 * h + 1024)])
         for f in ((pick_n, pick_d) if t == 0 else (pick_d, pick_n)):
             f()
         act(n_("ws"), ("p6", 0, 128), AF.Sign, bias=0.5)
         act(n_("wr"), n_("ws"), AF.Copy, scale=1920.0, bias=-1920.0)
         tt(tC, ("p6", 0, 128), n_("wr"), A.add)
-        tt(tA, n_("cS"), ("p6", 128, 256), A.mult)
+        tt(tA, n_("cS"), ("p2", 0, 128), A.mult)
         tt(n_("nN"), tA, n_("nF"), A.add)
         if not last:
             tt(n_("MN"), n_("nN"), OHA, A.mult)
@@ -450,9 +452,9 @@ def make(core, nxt, prv, T, topo):
         mm(o, [(o, CS(k), (n_("MV"), k, 128, 16)) for k in range(16)], ["CS", n_("MV")])
         ts(n_("VL"), o, 2048.0, A.add)
         act(n_("VF"), o, AF.Identity, bias=2048.0)
-        o = ("p5", 0, 128)
+        o = ("p1", 0, 128)
         mm(o, [(o, "BO", n_("MW"))], ["BO", n_("MW")])
-        op("a", lambda e, t=t: e.activation(ap("dl%d" % t), ap(("p5", 0, 128)), AF.Identity, bias=ap(("RTF", t, t + 1)), scale=ap(("RT8", t, t + 1))),
+        op("a", lambda e, t=t: e.activation(ap("dl%d" % t), ap(("p1", 0, 128)), AF.Identity, bias=ap(("RTF", t, t + 1)), scale=ap(("RT8", t, t + 1))),
            [o, "RTF", "RT8"], [n_("dl")], 0.18)
         for x in range(8):
             o = ("p%d" % (2 + x // 4), 128 * (x % 4), 128 * (x % 4) + 128)

from concourse.mybir import AluOpType as A, ActivationFunctionType as AF

NT = 3
TRASH = 1024
PB = ["p%d" % i for i in range(8)]
SCRATCH = {p: ("psum", [128, 512], "float32") for p in PB}
WHERE = {}


def _own(name, cols, dtype):
    SCRATCH[name] = ("sbuf", [128, cols], dtype)
    WHERE[name] = (name, 0, cols)


def _arena(buf, dtype, pieces):
    c = 0
    for name, w in pieces:
        WHERE[name] = (buf, c, w)
        c += (w + 15) // 16 * 16
    SCRATCH[buf] = ("sbuf", [128, c], dtype)


for _n, _w, _d in (("X", 4096 + TRASH, "bfloat16"), ("D", 4096, "bfloat16"), ("LM", 768, "bfloat16"), ("RT", 3, "bfloat16"), ("JT", 768, "int32"),
                   ("PK", 384, "int32"), ("JM", 8, "int32"), ("TL", 768, "float32"), ("NX", 768, "float32"), ("IB", 768, "int32"), ("IC", 768, "int32"),
                   ("ONE", 512, "bfloat16"), ("ZER", 512, "bfloat16"), ("BIG", 512, "bfloat16"), ("TRI", 512, "bfloat16"), ("EYE", 128, "bfloat16"),
                   ("EYE4", 128, "bfloat16"), ("NEYE", 128, "bfloat16"), ("NEYE8", 128, "bfloat16"), ("G8A", 8, "bfloat16"), ("G8", 8, "bfloat16"),
                   ("BOA", 128, "bfloat16"), ("BO", 128, "bfloat16"), ("GM", 1024, "bfloat16"), ("GMA", 1024, "bfloat16"), ("NGM", 1024, "bfloat16"),
                   ("CS", 144, "bfloat16"), ("DI", 2048, "bfloat16"), ("EX", 2048, "bfloat16"), ("RST", 256, "float32"), ("KC", 256, "bfloat16"),
                   ("GD", 16, "bfloat16"), ("MM", 8, "float32"), ("WI", 256, "float32"), ("WS", 256, "float32"), ("WF", 256, "float32"),
                   ("RTF", 3, "float32"), ("RT8", 3, "float32"), ("M3", 384, "float32"), ("PF", 384, "int32"), ("PG", 384, "float32"),
                   ("PM", 384, "int32"), ("YP", 384, "float32")):
    _own(_n, _w, _d)
for _t in range(NT):
    for _n, _w, _d in (("XA", 2048, "bfloat16"), ("OV", 2048, "bfloat16"), ("DG", 2048, "bfloat16"), ("N2", 2048, "float16"), ("GV", 128, "int32"),
                       ("LAND", 128, "int32")):
        _own("%s%d" % (_n, _t), _w, _d)
    SCRATCH["E3%d" % _t] = ("sbuf", [128, 8, 32], "bfloat16")
    SCRATCH["EE%d" % _t] = ("sbuf", [128, 8, 128], "bfloat16")
    _arena("u%d" % _t, "uint16", [("%s%d" % (n, _t), w) for n, w in (("JL", 8), ("aL", 128), ("nL", 128), ("VL", 8), ("OF", 8))])
    _arena("f%d" % _t, "float32", [("%s%d" % (n, _t), w) for n, w in (
        ("aF", 128), ("pm", 256), ("cS", 128), ("nN", 128), ("U", 128), ("Uc", 128), ("ms", 128), ("ux", 128), ("y1", 128), ("wr", 128), ("ab", 512),
        ("VF", 8), ("dl", 128), ("xg", 128), ("qn", 128), ("q", 128), ("w", 256), ("OFa", 8), ("OFb", 8))])
    _arena("i%d" % _t, "int32", [("%s%d" % (n, _t), w) for n, w in (("EQ", 128), ("evM", 128), ("evS", 128), ("M", 384), ("Q", 384))])
    _arena("b%d" % _t, "bfloat16", [("%s%d" % (n, _t), w) for n, w in (("Lj", 128), ("LT", 128), ("OH", 128), ("e", 384), ("r", 256), ("MW", 128), ("xc", 128),
                                                                       ("ws", 128))])
    _arena("h%d" % _t, "float16", [("%s%d" % (n, _t), w) for n, w in (("MN", 128), ("MV", 128), ("nF", 128))])
_arena("i%d" % NT, "int32", [("Q%d" % NT, 384)])
SEMAPHORES = ["v", "a", "t", "c"] + ["d%d" % i for i in range(24)] + ["arr%d" % t for t in range(NT)] + ["loc%d" % t for t in range(NT)]

XQ = ("avaa", "aaaa", "vaaa")
DQ = ("avva", "aaaa", "aaav")
NQ = ("vaaa", "aavv", "aaaa")
CQ = ("aa", "vv", "vv")
EB = ("va", "va", "va")
ORDER = ("nxd", "dxn", "dxn")
SEED = 128438
SPREAD = 0.6
WAKE = 0.10
TOL = 0.08
CYC = 0.83e-3
PEC = 0.42e-3


def build(ops, g, T):
    n = len(ops)
    acc = {}
    chain = {}
    soft = [None] * n
    pred = [[] for _ in range(n)]
    for i, o in enumerate(ops):
        ps = set()
        for buf, lo, hi, wr in o["acc"]:
            psum = buf in PB
            for j, lo2, hi2, wr2 in acc.setdefault(buf, []):
                if (lo < hi2 and lo2 < hi and (wr or wr2)) or (psum and ops[j]["q"] != o["q"]):
                    if not (o.get("grp") and o["grp"] == ops[j].get("grp")):
                        ps.add(j)
        for buf, lo, hi, wr in o["acc"]:
            acc[buf].append((i, lo, hi, wr))
        ps.discard(i)
        pred[i] = sorted(ps)
        o["pred"] = pred[i]
        k = o.get("line")
        if k:
            soft[i] = chain.get(k)
            chain[k] = i
    succ = [[] for _ in range(n)]
    left = [len(p) for p in pred]
    for i in range(n):
        for j in pred[i]:
            succ[j].append(i)
        if soft[i] is not None and soft[i] not in pred[i]:
            succ[soft[i]].append(i)
            left[i] += 1
    prio = [0.0] * n
    for i in range(n - 1, -1, -1):
        prio[i] = ops[i]["cost"] + ops[i]["lat"] + max([prio[s] + WAKE for s in succ[i]] + [0.0])
    h = SEED
    for i in range(n):
        h = (h * 1103515245 + 12345) % 2147483648
        if ops[i]["kind"] == "load":
            prio[i] = 1e6 - 1e3 * i
        else:
            prio[i] += SPREAD * (h / 2147483648.0)
    done = [None] * n
    free = {}
    link = [0.0]
    ready = {i for i in range(n) if not left[i]}
    order = []
    while ready:
        best = None
        ests = {}
        for i in ready:
            est = max([free.get(ops[i]["q"], 0.0)] + [done[j] + WAKE for j in pred[i]])
            ests[i] = est
            if best is None or est < ests[best] or (est == ests[best] and i < best):
                best = i
        q = ops[best]["q"]
        lim = ests[best] + TOL
        pick = max((i for i in ready if ops[i]["q"] == q and ests[i] <= lim), key=lambda i: (prio[i], -i))
        ready.discard(pick)
        o = ops[pick]
        st = ests[pick]
        free[q] = st + o["cost"]
        if o["kind"] in ("load", "dma"):
            link[0] = max(link[0], st + 1.3) + o["bytes"] / 250e3
            done[pick] = link[0] + 0.7
        else:
            done[pick] = st + o["cost"] + o["lat"]
        o["when"] = (st, done[pick])
        o["pos"] = len(order)
        order.append(pick)
        for s in succ[pick]:
            left[s] -= 1
            if not left[s]:
                ready.add(s)
    eng = {"v": g.vector, "a": g.scalar, "t": g.tensor, "c": g, "s": g.sync}
    known = {q: {} for q in eng}
    count = {q: 0 for q in eng}
    comp = [None] * n
    clock = [None] * n
    total = {}
    nd = 0
    for i in order:
        o = ops[i]
        q = o["q"]
        if o["kind"] == "arrive":
            comp[i] = (o["sem"], o["val"])
            clock[i] = {}
            total[o["sem"]] = o["val"]
            continue
        kn = known[q]
        need = {}
        for j in pred[i]:
            s, v = comp[j]
            if kn.get(s, 0) < v and need.get(s, (0, 0))[0] < v:
                need[s] = (v, j)
        for s in sorted(need, key=lambda s: -need[s][1]):
            v, j = need[s]
            if kn.get(s, 0) >= v:
                continue
            eng[q].wait_ge(T.sem[s], v)
            kn[s] = v
            for s2, v2 in clock[j].items():
                if kn.get(s2, 0) < v2:
                    kn[s2] = v2
        clock[i] = dict(kn)
        if o["kind"] in ("load", "dma"):
            s = "d%d" % nd
            nd += 1
            o["fns"][0](eng[q]).then_inc(T.sem[s], 16)
            comp[i] = (s, 16)
        elif o["kind"] == "remote":
            o["fns"][0](g)
            comp[i] = (o["sem"], o["val"])
        else:
            for f in o["fns"]:
                f(eng[q]).then_inc(T.sem[q], 1)
            count[q] += len(o["fns"])
            comp[i] = (q, count[q])
        total[comp[i][0]] = comp[i][1]
    for s in sorted(total):
        if known["c"].get(s, 0) < total[s]:
            g.wait_ge(T.sem[s], total[s])
    return max(d for d in done if d is not None)


def rank_program(g, core, T, topo):
    rank = T.rank_of(core)
    if rank is None:
        return
    nxt = T.cores[(rank + 1) % len(T.cores)]
    prv = T.cores[(rank - 1) % len(T.cores)]
    build(make(core, nxt, prv, T, topo), g, T)


def make(core, nxt, prv, T, topo):
    ops = []

    def norm(x):
        x = (x,) if isinstance(x, str) else x
        buf, c0, w = WHERE.get(x[0], (x[0], 0, 512))
        lo, hi = (x[1], x[2]) if len(x) > 1 else (0, w)
        return buf, c0 + lo, c0 + hi, (x[3] if len(x) > 3 else 1)

    def ap(x):
        if isinstance(x, list):
            return x[0]()
        buf, lo, hi, st = norm(x)
        return T[buf][:, lo:hi:st] if st > 1 else T[buf][:, lo:hi]

    def reg(x, wr):
        if x[:2] in ("E3", "EE"):
            return (x, 0, 9999, wr)
        return norm(x)[:3] + (wr,)

    def op(q, fns, R, W, cost, kind="op", lat=0.0, **kw):
        o = {"q": q, "fns": fns if isinstance(fns, list) else [fns], "acc": [reg(x, False) for x in R] + [reg(x, True) for x in W], "cost": cost,
             "kind": kind, "lat": lat}
        o.update(kw)
        ops.append(o)

    def width(x):
        _, lo, hi, st = norm(x)
        return (hi - lo + st - 1) // st

    def isps(x):
        return (x if isinstance(x, str) else x[0]) in PB

    def vc(c):
        return 0.05 + max(64, c) * CYC

    def tt(out, a, b, o):
        op("v", lambda e: e.tensor_tensor(ap(out), ap(a), ap(b), o), [a, b], [out], vc(width(a) * (1 if isps(a) or isps(b) else 2)))

    def ts(out, a, s1, o1, s2=None, o2=None):
        f = (lambda e: e.tensor_scalar(ap(out), ap(a), s1, None, o1)) if o2 is None else (lambda e: e.tensor_scalar(ap(out), ap(a), s1, s2, o1, o2))
        op("v", f, [a], [out], vc(width(a)))

    def cp(q, out, a):
        if q == "v":
            op("v", lambda e: e.tensor_copy(ap(out), ap(a)), [a], [out], vc(width(a) * 0.5))
        else:
            act(out, a, AF.Copy)

    def act(out, a, f, **kw):
        op("a", lambda e: e.activation(ap(out), ap(a), f, **kw), [a], [out], 0.07 + max(64, width(a)) * CYC)

    def gather(q, out, win, w, lst, line=None):
        n = 16 * width(lst)
        if q == "v":
            op("v", lambda e: e.tensor_copy(ap(out), T[win][:, 0:w].indirect(ap(lst))), [(win, 0, w), lst], [out], 0.05 + n * 1.5 * CYC, line=line and line + q)
        else:
            op("a", lambda e: e.activation(ap(out), T[win][:, 0:w].indirect(ap(lst)), AF.Copy), [(win, 0, w), lst], [out], 0.065 + n * 1.5 * CYC,
               line=line and line + q)

    def scatter(win, w, lst, val):
        op("v", lambda e: e.tensor_copy(T[win][:, 0:w].indirect(ap(lst)), ap(val)), [lst, val], [(win, 0, w)], 0.05 + 16 * width(lst) * 3 * CYC)

    def mm(out, parts, rd, start=True, stop=True, each=False, grp=None):
        k = len(parts)
        fns = [(lambda e, i=i, a=a: e.matmul(ap(a[0]), ap(a[1]), ap(a[2]), each or (start and i == 0), each or (stop and i == k - 1))) for i, a in enumerate(parts)]
        op("t", fns, list(rd), [out], sum(max(64, width(a[2])) for a in parts) * PEC + 0.01 * k, grp=grp, line=grp)

    def load(dst, src, nbytes, lo=0, hi=None):
        op("s", lambda e: e.dma_start(ap(dst), T[src][:, lo:hi] if hi else T[src][:]), [], [dst], 0.06, kind="load", bytes=nbytes)

    def fill(x, val):
        op("v", lambda e: e.memset(ap(x), val), [], [x], vc(width(x) * 0.5))

    def sel(out, a, pat, base, cm, cmp=A.is_ge, other=0.0):
        op("c", lambda e: e.affine_select(ap(out), ap(a), pat, cmp, other, base, cm), [a], [out], 0.17 + 2 * width(out) * CYC)

    def iota(out, pat, base, cm):
        op("c", lambda e: e.iota(ap(out), pat, base, cm, allow_small_or_imprecise_dtypes=True), [], [out], 0.13 + 2 * width(out) * CYC)

    load("JM", "jm", 4096)
    load("JT", "jt", 128 * 768 * 4)
    load(("D", 3840, 4096), "sd", 64 << 10, 3840, 4096)
    load("RT", "rt", 768)
    load("LM", "lm", 128 * 768 * 2)
    load(("X", 0, 4096), "xw", 1 << 20)
    load("PK", "pk", 128 * 384 * 4)
    load(("D", 0, 3840), "sd", 960 << 10, 0, 3840)

    fill("ONE", 1.0)
    fill("BIG", 8192.0)
    sel("EYE", ("ONE", 0, 128), [[-1, 128]], 0, 1, A.is_equal)
    sel("G8A", ("ONE", 0, 8), [[-16, 8]], 0, 1)
    sel("G8", "G8A", [[16, 8]], 15, -1)
    sel("BOA", ("ONE", 0, 128), [[-16, 8], [0, 16]], 0, 1)
    sel("BO", "BOA", [[16, 8], [0, 16]], 15, -1)
    iota("KC", [[0, 16], [-1, 16]], 15, 0)
    iota("MM", [[128, 8]], 4096, 1)
    sel("TRI", "BIG", [[0, 4], [-1, 128]], 0, 1)
    iota("WI", [[1, 256]], 3840, 0)
    fill("RST", 1.0)
    fill(("RST", 0, 256, 32), 0.0)
    fill("CS", 0.0)
    cp("v", ("CS", 15, 143, 16), "G8")
    fill("DI", 0.0)
    fill("ZER", 0.0)
    for h in range(4):
        sel(("EX", 512 * h, 512 * h + 512), "ZER", [[-1, 32], [0, 16]], -32 * h, 1, A.not_equal, 1.0)
    ts(("GD", 0, 16, 2), "G8", 16.0, A.mult)
    ts(("GD", 1, 16, 2), "G8", 16.0, A.mult)
    for k in range(16):
        cp("a", ("DI", k * 128 + k, k * 128 + 128, 16), ("EYE", k, 128, 16))
    for h in range(2):
        x = ("GMA", 512 * h, 512 * h + 512)
        sel(x, "ONE", [[-16, 4], [0, 128]], -64 * h, 1)
        sel(("GM", 512 * h, 512 * h + 512), x, [[16, 4], [0, 128]], 64 * h + 15, -1)
    act("NGM", "GM", AF.Copy, scale=-1.0)
    act("EYE4", "EYE", AF.Copy, scale=4.0)
    act("NEYE", "EYE", AF.Copy, scale=-1.0)
    act("NEYE8", "EYE", AF.Copy, scale=-8.0)

    def CS(k):
        return ("CS", 15 - k, 143 - k)

    def DI(k):
        return ("DI", 128 * k, 128 * k + 128)

    cp("v", "JL0", "JM")
    ts("IC", "JT", 4095, A.bitwise_and)
    cp("v", "TL", "IC")
    ts("IB", "JT", 12, A.logical_shift_right)
    cp("v", "NX", "IB")
    we = ("D", 3840, 4096)
    tt("WS", we, "WI", A.add)
    ts("WF", "WS", 4096.0, A.is_ge, -256.0, A.mult)
    tt(we, we, "WF", A.add)
    cp("v", "RTF", "RT")
    ts("RT8", "RT", -1.0, A.mult, -8.0, A.add)
    ts("M0", "PK", 4095, A.bitwise_and)
    ts("M3", "M0", -3.0, A.mult)
    for i in range(3):
        ts(("PG", 128 * i, 128 * i + 128), ("PK", 128 * i, 128 * i + 128), 4.0, A.mult, 4096.0 * (2 - i), A.add)
    tt("Q0", "PG", "M3", A.add)

    for t in range(NT):
        def n_(x, t=t):
            return "%s%d" % (x, t)
        last = t == NT - 1
        JL, aL, nL, XA, OV, DG, N2 = (n_(x) for x in ("JL", "aL", "nL", "XA", "OV", "DG", "N2"))
        Q2 = ("Q0", 256, 384) if t == 0 else "LAND%d" % (t - 1)
        Q0, Q1, Q01 = (n_("Q"), 0, 128), (n_("Q"), 128, 256), (n_("Q"), 0, 256)
        tA, tB, tC, tD = (("p7", 128 * i, 128 * i + 128) for i in range(4))
        tCD = ("p7", 256, 512)
        OHA = ("p4", 256, 384)
        gather("v", aL, "TL", 768, JL)
        gather("a", n_("Lj"), "LM", 768, JL)
        gather("v", nL, "NX", 768, JL)
        gather("a", n_("aF"), "TL", 768, JL)
        gather("a", n_("nF"), "NX", 768, JL)
        o = ("p0", 0, 128)
        mm(o, [(o, n_("Lj"), "EYE")], [n_("Lj"), "EYE"])
        cp("a", n_("LT"), o)

        def wear():
            for q, e in enumerate(XQ[t]):
                gather(e, (XA, 512 * q, 512 * q + 512), "X", 4096, (aL, 32 * q, 32 * q + 32), "g%d" % t)

        def dist():
            for q, e in enumerate(DQ[t]):
                gather(e, (DG, 512 * q, 512 * q + 512), "D", 4096, (aL, 32 * q, 32 * q + 32), "g%d" % t)

        def second():
            for q, e in enumerate(NQ[t]):
                gather(e, (N2, 512 * q, 512 * q + 512), "NX", 768, (nL, 32 * q, 32 * q + 32), "g%d" % t)
        for y in ORDER[t]:
            {"d": dist, "n": second, "x": wear}[y]()
        for q in range(4):
            c, b = (XA, 512 * q, 512 * q + 512), "p%d" % (q // 2)
            o, x = (OV, 512 * q, 512 * q + 512), ("EX", 512 * q, 512 * q + 512)
            if CQ[t][q // 2] == "v":
                mm(b, [(b, n_("LT"), x)], [n_("LT"), x])
                tt(o, c, b, A.is_gt)
            else:
                mm(b, [(b, n_("LT"), x), (b, "NEYE", c)], [n_("LT"), x, "NEYE", c])
                act(o, b, AF.Sign, scale=-1.0, bias=-0.5)
        k2 = ("p4", 0, 256)
        mm(k2, [(k2, "EYE", "KC")], ["EYE", "KC"], stop=False, grp="k%d" % t)
        mm(k2, [(("p4", k, 256, 16), (XA, k, 2048, 16), "GD") for k in range(16)], [XA, "GD"], start=False, grp="k%d" % t)
        op("v", lambda e, x=n_("pm"): e.tensor_tensor_scan(ap(x), ap("RST"), ap(("p4", 0, 256)), 0.0, A.mult, A.max), ["RST", k2], [n_("pm")], vc(256))
        op("v", lambda e, t=t: e.tensor_tensor(T["E3%d" % t][:, :, :], ap(("p4", 0, 256)), ap("pm%d" % t), A.is_equal), [k2, n_("pm")], ["E3%d" % t], vc(256))
        op("a", lambda e, t=t: e.activation(ap("OH%d" % t), T["E3%d" % t][:, :, 16:32], AF.Copy), ["E3%d" % t], [n_("OH")], 0.18)
        mm(OHA, [(OHA, n_("OH"), "EYE")], [n_("OH"), "EYE"])
        for h in range(2):
            o = ("p5", 64 * h, 64 * h + 64)
            mm(o, [(o, CS(k), (OV, 1024 * h + k, 1024 * h + 1024, 16)) for k in range(16)], ["CS", (OV, 1024 * h, 1024 * h + 1024)])
        for h in range(2):
            ts((n_("cS"), 64 * h, 64 * h + 64), ("p5", 64 * h, 64 * h + 64), 8.5 if CQ[t][h] == "v" else 1.0, A.is_ge)

        def pick_n():
            for h in range(2):
                o = ("p2", 64 * h, 64 * h + 64)
                mm(o, [(o, DI(k), (N2, 1024 * h + k, 1024 * h + 1024, 16)) for k in range(16)] + [(o, "NEYE", (n_("nF"), 64 * h, 64 * h + 64))],
                   ["DI", (N2, 1024 * h, 1024 * h + 1024), "NEYE", n_("nF")])

        def pick_d():
            for h in range(2):
                o = ("p6", 64 * h, 64 * h + 64)
                mm(o, [(o, DI(k), (DG, 1024 * h + k, 1024 * h + 1024, 16)) for k in range(16)], ["DI", (DG, 1024 * h, 1024 * h + 1024)])
        for f in ((pick_n, pick_d) if t == 0 else (pick_d, pick_n)):
            f()
        act(n_("ws"), ("p6", 0, 128), AF.Sign, bias=0.5)
        act(n_("wr"), n_("ws"), AF.Copy, scale=1920.0, bias=-1920.0)
        tt(tC, ("p6", 0, 128), n_("wr"), A.add)
        tt(tA, n_("cS"), ("p2", 0, 128), A.mult)
        tt(n_("nN"), tA, n_("nF"), A.add)
        if not last:
            tt(n_("MN"), n_("nN"), OHA, A.mult)
            mm(("p4", 0, 8), [(("p4", 0, 8), CS(k), (n_("MN"), k, 128, 16)) for k in range(16)], ["CS", n_("MN")])
            cp("v", "JL%d" % (t + 1), ("p4", 0, 8))
            scatter("NX", 768, JL, n_("nN"))
        tt(tC, n_("cS"), tC, A.mult)
        tt(tB, tC, n_("aF"), A.add)
        tt(n_("U"), tC, n_("aF"), A.add)
        act(n_("Uc"), n_("U"), AF.Identity, bias=-2048.0)
        if not last:
            scatter("TL", 768, JL, n_("U"))
        if t:
            ts((n_("M"), 256, 384), Q2, 4095, A.bitwise_and)
        tt(tD, Q0, Q1, A.max)
        tt(n_("EQ"), tD, Q2, A.max)
        r0, r1 = (n_("r"), 0, 128), (n_("r"), 128, 256)
        tt(r0, Q0, n_("EQ"), A.is_equal)
        tt(r1, Q1, n_("EQ"), A.is_equal)
        ts(n_("evM"), n_("EQ"), 4095, A.bitwise_and)
        ts(n_("evS"), n_("EQ"), 0xFFCFFF, A.bitwise_and)
        tt(tD, n_("evS"), Q2, A.subtract)
        e0, e1, e2 = ((n_("e"), 128 * i, 128 * i + 128) for i in range(3))
        for i, x in enumerate((e0, e1, e2)):
            tt(x, (n_("M"), 128 * i, 128 * i + 128), tB, A.is_equal)
        o = ("p5", 128, 256)
        mm(o, [(o, "EYE", e0), (o, "EYE", e1), (o, "EYE", e2)], ["EYE", n_("e")])
        act(n_("ms"), o, AF.Relu, scale=-1.0, bias=1.0)
        tt(n_("ux"), n_("evM"), tB, A.subtract)
        tt(tC, n_("ux"), OHA, A.mult)
        tt(n_("y1"), n_("Uc"), OHA, A.mult)
        tt(tC, n_("ms"), tC, A.mult)
        tt(n_("MV"), tC, n_("y1"), A.add)
        tt(n_("MW"), n_("ms"), OHA, A.mult)
        for b in range(2):
            o = "p%d" % (2 + b)
            mm(o, [(o, "EYE", "TRI")], ["EYE", "TRI"], stop=False, grp="e%d%d" % (t, b))
            mm(o, [(o, n_("MV"), ("NGM", 512 * b, 512 * b + 512))] +
               [((o, 128 * x, 128 * x + 128), ("GM", 128 * (4 * b + x), 128 * (4 * b + x) + 128), n_("MV")) for x in range(4)],
               [n_("MV"), "NGM", "GM"], start=False, grp="e%d%d" % (t, b))
        o = ("p4", 8, 16)
        mm(o, [(o, CS(k), (n_("MV"), k, 128, 16)) for k in range(16)], ["CS", n_("MV")])
        ts(n_("VL"), o, 2048.0, A.add)
        act(n_("VF"), o, AF.Identity, bias=2048.0)
        o = ("p1", 0, 128)
        mm(o, [(o, "BO", n_("MW"))], ["BO", n_("MW")])
        op("a", lambda e, t=t: e.activation(ap("dl%d" % t), ap(("p1", 0, 128)), AF.Identity, bias=ap(("RTF", t, t + 1)), scale=ap(("RT8", t, t + 1))),
           [o, "RTF", "RT8"], [n_("dl")], 0.18)
        for x in range(8):
            o = ("p%d" % (2 + x // 4), 128 * (x % 4), 128 * (x % 4) + 128)
            if EB[t][x // 4] == "v":
                op("v", lambda e, x=x, t=t, o=o: e.tensor_scalar(T["EE%d" % t][:, :, 16 * x:16 * x + 16], ap(o), 0.0, None, A.is_equal), [o], [], 0.16)
            else:
                if x % 4 == 0:
                    act(n_("ab"), "p%d" % (2 + x // 4), AF.Abs)
                o = (n_("ab"), 128 * (x % 4), 128 * (x % 4) + 128)
                op("a", lambda e, x=x, t=t, o=o: e.activation(T["EE%d" % t][:, :, 16 * x:16 * x + 16], ap(o), AF.Relu, scale=-1.0, bias=1.0), [o], [], 0.18)
            ops[-1]["acc"].append(("EE%d" % t, x, x + 1, True))
        op("v", lambda e, t=t: e.tensor_tensor(ap("xg%d" % t), T.X[:, 0:4096].indirect(ap("VL%d" % t)), ap("dl%d" % t), A.add),
           [("X", 0, 4096), n_("VL"), n_("dl")], [n_("xg")], 0.22)
        ts(n_("xc"), n_("xg"), 0.0, A.max, 255.0, A.min)
        o = ("p4", 16, 24)
        mm(o, [(("p4", 16 + c, 17 + c), [lambda c=c, t=t: T["EE%d" % t][:, c, :]], ("BIG", 0, 1)) for c in range(8)], ["EE%d" % t, "BIG"], each=True)
        tt(n_("OFa"), o, "MM", A.min)
        tt(n_("OFb"), n_("OFa"), n_("VF"), A.max)
        cp("v", n_("OF"), n_("OFb"))
        scatter("X", 4096 + TRASH, n_("OF"), n_("xc"))
        tt(tD, n_("ms"), tD, A.mult)
        tt(n_("GV"), tD, Q2, A.add)
        out = topo.engines(core, nxt)[:8]
        rin = topo.engines(prv, core)[:8]
        rid, pid = topo.addr(nxt)[:2]
        op("c", lambda e, t=t, rid=rid, pid=pid, m=sum(1 << x for x in out): e.remote_dma(
            T["LAND%d" % t][:], T["GV%d" % t][:], T.sem["arr%d" % t], T.sem["loc%d" % t], pid, rid, m),
           [n_("GV")], [("SENT%d" % t, 0, 1)], 0.3, kind="remote", lat=2.0, sem="loc%d" % t, val=len(out))
        op("z%d" % t, None, [("SENT%d" % t, 0, 1)], ["LAND%d" % t], 0.0, kind="arrive", lat=2.0, sem="arr%d" % t, val=len(rin))
        act(n_("qn"), n_("nN"), AF.Copy, scale=16384.0)
        tt(n_("q"), n_("qn"), tB, A.add)
        act(("p3", 0, 128), n_("q"), AF.Identity, bias=8192.0)
        act(("p3", 128, 256), n_("q"), AF.Identity, bias=4096.0)
        o = ("p5", 256, 384)
        mm(o, [(o, "EYE4", e0), (o, "NEYE", e1), (o, "NEYE", e2), (o, "EYE", r0)], ["EYE4", "NEYE", "EYE", n_("e"), n_("r")])
        o = ("p5", 384, 512)
        mm(o, [(o, "NEYE8", e0), (o, "EYE4", e1), (o, "NEYE", e2), (o, "EYE", r1)], ["EYE4", "NEYE8", "NEYE", "EYE", n_("e"), n_("r")])
        ts(n_("w"), ("p5", 256, 512), 0.5, A.is_ge)
        tt(tCD, ("p3", 0, 256), Q01, A.subtract)
        tt(tCD, n_("w"), tCD, A.mult)
        tt(("Q%d" % (t + 1), 0, 256), tCD, Q01, A.add)
        if not last:
            ts(("M%d" % (t + 1), 0, 256), ("Q%d" % (t + 1), 0, 256), 4095, A.bitwise_and)

    for src, lo, hi in ((("Q%d" % NT, 0, 256), 0, 256), ("LAND%d" % (NT - 1), 256, 384)):
        ts(("PF", lo, hi), src, 0xFFC000, A.bitwise_and)
        ts(("PM", lo, hi), src, 4095, A.bitwise_and)
        ts(("PG", lo, hi), ("PF", lo, hi), 0.25, A.mult)
        tt(("YP", lo, hi), ("PG", lo, hi), ("PM", lo, hi), A.add)
    op("s", lambda e: e.dma_start(T.yx[:], ap(("X", 0, 4096))), [("X", 0, 4096)], [("OUTX", 0, 1)], 0.06, kind="dma", bytes=1 << 20, lat=7.0)
    op("s", lambda e: e.dma_start(T.yp[:], ap("YP")), ["YP"], [("OUTP", 0, 1)], 0.06, kind="dma", bytes=128 * 384 * 4, lat=3.0)
    return ops
